import numpy as np, ml_dtypes
CORES = [35,38,43,46]
N = 4
BF = ml_dtypes.bfloat16
C, P, WA, WM, MC, RO = 128, 32, 4096, 2048, 16, 3
L0, LM, AM, Q, B = 4, 15, 7, 2048 // 128, 16 // 16
def block(rng, n):
    q = rng.integers(24, 257, (N, 8, 16, n // P, 1))
    return (rng.random((N, 8, 16, n // P, P)) * q).astype(np.int64).reshape(N, 8, 16, n)
def parts(rng):
    X = block(rng, C * P); A = block(rng, WA); M = rng.integers(0, 256, (N, 8, 16, WM))
    w = rng.integers(0, 256, (N, 8, 16, 2)); k = rng.integers(0, 2048, (N, 8, 2, MC))
    t = np.stack([rng.integers(700, 1101, (N, 8)), rng.integers(700, 1001, (N, 8))], axis=2)
    return X, A, M, w, k, t
def pack(X, A, M, w, k, t):
    b = lambda v: np.ascontiguousarray(v.reshape(N, 128, -1)).astype(np.float32).astype(BF)
    h = k.reshape(N, 8, 2, B, 16).transpose(0, 1, 4, 2, 3).reshape(N, 128, 2 * B)
    return {"gn": b(X), "ar": b(A), "mh": b(M), "wt": b(w), "hk": np.ascontiguousarray(h).astype(np.int32), "th": np.repeat(t, 16, axis=1).astype(np.int32)}
def setup_inputs(rng):
    return pack(*parts(rng))
def setup_inputs_ties(rng):
    X, A, M, w, k, t = parts(rng)
    return pack((X >> 4) << 4, (A >> 4) << 4, (M >> 4) << 4, w | 1, k, (t >> 4) << 4)
def setup_inputs_ends(rng):
    X, A, M, w, k, t = parts(rng); E = X.reshape(N, 8, 16, C, P); c = np.arange(C); uu = np.arange(4096)
    k[:, 1::2, :, 0] = 0; k[:, 1::2, :, MC - 1] = 2047
    for q in range(N):
        for g in range(0, 8, 2):
            o = (2 * rng.permutation(2048)[:64] + 1) | (LM << 4)
            s = ((o * o >> 5)[:, None] + o[:, None] * np.arange(2048)[None, :]) & (WA - 1)
            j = int(np.argmax(s)); key = j % 2048; k[q, g, 0] = key
            near = np.argsort(((uu * uu >> 5) + key * uu) & (WA - 1))[-64:]
            u = near[rng.integers(0, 64, C)]; u[0] = 0; u[1] = o[j // 2048]; u[C - 1] = o[j // 2048]
            w[q, g, :, 0] = 0; w[q, g, 0, 0] = 1; w[q, g, 1, 0] = 128
            E[q, g, 0, c, c & AM] = u & 127; E[q, g, 1, c, c & AM] = u >> 7
    t[:, ::2, 0] = 4096; t[:, 0, 1] = 0
    return pack(E.reshape(N, 8, 16, C * P), A, M, w, k, t)
def setup_inputs_edges(rng):
    X, A, M, w, k, t = parts(rng)
    t[:, 0, 0] = 0; t[:, 1, 1] = 4096; t[:, 2, 0] = 4096; t[:, 2, 1] = 0; t[:, 3] = 1
    pat = rng.integers(0, 256, (16, 2)); pat[0, 0] = 3; pat[0, 1] = 200
    X[:, 3] = np.where(rng.random((N, 1, C * P)) < 0.5, pat[None, :, :1], pat[None, :, 1:])
    A[:, 3] = np.where(rng.random((N, 1, WA)) < 0.5, pat[None, :, :1], pat[None, :, 1:])
    M[:, 3] = np.where(rng.random((N, 1, WM)) < 0.06, np.max(pat, axis=1)[None, :, None], M[:, 3])
    w[:, 4] = rng.integers(240, 256, (N, 16, 2))
    X[:, 4] = rng.integers(200, 256, (N, 16, C * P)); A[:, 4] = rng.integers(200, 256, (N, 16, WA)); M[:, 4] = rng.integers(200, 256, (N, 16, WM))
    t[:, 4, 0] = rng.integers(230, 331, N); t[:, 4, 1] = rng.integers(230, 301, N)
    for g, lo in ((5, 150), (7, 70)):
        lev = int(rng.integers(lo, 241))
        X[:, g] = rng.integers(0, 16, (N, 16, C * P)) + (lev if g == 7 else 0)
        A[:, g] = rng.integers(0, 16, (N, 16, WA)) + (lev if g == 5 else 0)
        M[:, g] = rng.integers(0, 16, (N, 16, WM))
        t[:, g, 0] = 16 * lev + 4 * rng.integers(-5, 6, N) + rng.integers(0, 2, N)
        t[:, g, 1] = 16 * lev + 4 * rng.integers(10, 19, N) + rng.integers(0, 2, N)
    pa = rng.integers(0, 256, (16, 8))
    jx = np.repeat(rng.integers(0, 8, (N, C)), P, axis=1); ja = np.repeat(rng.integers(0, 8, (N, WA // P)), P, axis=1)
    jx = np.where((np.arange(C * P) // P) % 8 < 4, jx, rng.integers(0, 8, (N, C * P)))
    X[:, 6] = pa[:, jx].transpose(1, 0, 2); A[:, 6] = pa[:, ja].transpose(1, 0, 2)
    t[:, 6, 0] = 1; t[:, 6, 1] = 0
    return pack(X, A, M, w, k, t)
def setup_inputs_alike(rng):
    X, A, M, w, k, t = parts(rng); E = X.reshape(N, 8, 16, C, P); H = A.reshape(N, 8, 16, WA // P, P)
    E[:, ::2] = np.repeat(E[:, ::2, :, :1], C, axis=3); E[:, :, :, 5::8] = 0
    H[:, 1::2] = np.tile(H[:, 1::2, :, :4], (1, 1, 1, WA // P // 4, 1))
    M[:, 3::4] = M[:, 3::4][..., rng.integers(0, 8, WM)]
    k[..., 1::2] = k[..., ::2]
    return pack(E.reshape(N, 8, 16, C * P), H.reshape(N, 8, 16, WA), M, w, k, t)
def setup_inputs_spread(rng):
    X, A, M, w, k, t = parts(rng)
    X = (np.exp2(8 * rng.random((N, 8, 1, C * P))) * rng.random(X.shape)).astype(np.int64)
    A = (np.exp2(8 * rng.random((N, 8, 1, WA))) * rng.random(A.shape)).astype(np.int64)
    M = (np.exp2(4 + 4 * rng.random((N, 8, 1, WM))) * (0.5 + 0.5 * rng.random(M.shape))).astype(np.int64)
    w = np.exp2(8 * rng.random(w.shape)).astype(np.int64); k = np.exp2(11 * rng.random(k.shape)).astype(np.int64)
    t = np.stack([np.exp2(6.5 + 3.5 * rng.random((N, 8))), np.exp2(9 + 2 * rng.random((N, 8)))], axis=2).astype(np.int64)
    return pack(np.minimum(X, 255), np.minimum(A, 255), np.minimum(M, 255), np.minimum(w, 255), np.minimum(k, 2047), t)
def check_inputs(d):
    bad = []
    for s in ("gn", "ar", "mh", "wt"):
        v = d[s].astype(np.float32)
        if not (np.all(v >= 0) and np.all(v <= 255) and np.all(v == np.floor(v))): bad.append("whole numbers from 0 to 255 in " + s)
    for s, hi in (("hk", 2047), ("th", 4096)):
        if np.min(d[s]) < 0 or np.max(d[s]) > hi: bad.append("range of " + s)
    v = d["th"].reshape(N, 8, 16, 2)
    if not np.all(v == v[:, :, :1]): bad.append("th alike in the rows of a group")
    return bad
def pick(a, ix):
    return np.take_along_axis(a, ix.reshape(N, 8, 1, -1), 3).reshape((N, 8, 16) + ix.shape[2:])
def reference(gn, ar, mh, wt, hk, th):
    ints = lambda v: v.astype(np.float32).astype(np.int64)
    X = ints(gn).reshape(N, 8, 16, C, P); A = ints(ar).reshape(N, 8, 16, WA); M = ints(mh).reshape(N, 8, 16, WM); w = ints(wt).reshape(N, 8, 16, 2)
    k = hk.astype(np.int64).reshape(N, 8, 16, 2, B).transpose(0, 1, 3, 4, 2).reshape(N, 8, 2, MC)
    lim = th.astype(np.int64).reshape(N, 8, 16, 2)[:, :, 0, :, None, None]
    c = np.arange(C); m = np.arange(MC); i = np.arange(P)
    for t in range(RO):
        d = 1 + t % (N - 1); a = (c + 3 * t) & AM
        xa = X[:, :, :, c, a]
        u = np.add.reduce(w[..., 0:1] * xa, axis=2) & 4095
        p = ((u * u >> 5)[..., None] + k[:, :, 0, None, :] * u[..., None]) & (WA - 1)
        l = L0 + ((u[..., None] * (2 * m + 1) >> 4) & LM)
        d1 = np.add.reduce(np.abs(pick(A, p) - xa[..., None]), axis=2)
        xe = pick(X.reshape(N, 8, 16, C * P), (P * c + a)[:, None] + l)
        d2 = np.add.reduce(np.abs(pick(A, (p + l) & (WA - 1)) - xe), axis=2)
        score = np.where((d1 < lim[:, :, 0]) & (d2 < lim[:, :, 0]), l * MC + (MC - 1 - m), -1)
        best = np.argmax(score, axis=3)[..., None]
        lb = np.where(np.max(score, axis=3)[..., None] >= 0, np.take_along_axis(l, best, 3), 0); pb = np.take_along_axis(p, best, 3)
        inside = (i > a[:, None]) & (i < a[:, None] + lb)
        trial = np.where(inside[:, :, None], pick(A, (pb + i - a[:, None]) & (WA - 1)), X)
        z = np.roll(np.max(trial, axis=4), d, axis=0)
        v = np.add.reduce(w[..., 1:2] * z, axis=2) & 4095
        pm = ((v * v >> 5)[..., None] + k[:, :, 1, None, :] * v[..., None]) & (WM - 1)
        dm = np.add.reduce(np.abs(pick(M, pm) - z[..., None]), axis=2)
        known = np.any(dm < lim[:, :, 1], axis=3)
        np.put_along_axis(M, (C * (v & (Q - 1)) + c)[:, :, None, :], z, 3)
        new = np.roll(np.logical_not(known), -d, axis=0)
        X = np.where(new[:, :, None, :, None], trial, X)
        over = new & ((c & 3) == (t & 3))
        head = np.where(over[:, :, None, :, None], trial, A[..., :C * P].reshape(N, 8, 16, C, P))
        A = np.concatenate([head.reshape(N, 8, 16, C * P), A[..., C * P:]], axis=3)
    return {"y": np.ascontiguousarray(X).reshape(N, 128, C * P).astype(np.float32).astype(BF)}

@@ -1,0 +1,706 @@
+from concourse.bass import DstId, RemoteDMATransfer
+from concourse.mybir import AluOpType, ActivationFunctionType
+
+ALU = AluOpType
+ACT = ActivationFunctionType
+
+NR = 4
+RO = 3
+n = 64
+NCH = 2
+SPLIT_D = True
+XOFF, AOFF, PAD, WEND = 12288, 16384, 20480, 20512
+BIG = float(2 ** 22)
+ES = float(2 ** 25)
+
+CFG = {"tg": [512, 512, 512, 512], "delta": 60.0, "bias": 1000.0, "pen": 3000.0,
+       "steps": [5, 10, 12, 47, 52, 53, 78, 104, 114, 117, 131, 139, 200, 206, 216, 218, 316, 358, 425, 490, 511, 538]}
+
+SCRATCH = {}
+SEMAPHORES = ["cV", "cS", "cP", "cG", "sent"]
+for _dt, _list in [
+    ("bfloat16", [("W", WEND), ("Y", 4096), ("Mo", 2048), ("M0", 2048), ("M1", 2048), ("M2", 2048), ("wtb", 8),
+                  ("ones", 128), ("blk0", 128), ("blk", 128), ("idn", 128), ("nidn", 128), ("bk", 128), ("bkn", 128),
+                  ("wb", 128), ("tb", 128), ("wj", 384), ("zs", 144), ("zw", 288), ("c32b", 128), ("cst", 192),
+                  ("m32", 1024), ("tmp", 1024), ("zc0", 128), ("zc1", 128), ("zl0", 128), ("zl1", 128), ("zl2", 128)]),
+    ("float32", [("PF", 8), ("PR0", 8), ("PR1", 8), ("PR2", 8), ("c32", 128), ("c32p", 128), ("af", 264),
+                 ("jt", 528), ("cf", 16), ("m16", 64), ("q16", 8), ("sf", 16)]),
+    ("int32", [("hki", 4), ("thi", 4), ("ai", 264), ("ci", 80), ("si", 16)]),
+    ("uint16", [("xoff", 48), ("yo", 256), ("so0", 8), ("so1", 8), ("sl0", 8), ("sl1", 8), ("sl2", 8)]),
+]:
+    for _nm, _cols in _list:
+        SCRATCH[_nm] = ("sbuf", [128, _cols], _dt)
+for _h in range(NCH):
+    for _nm, _cols, _dt in [
+        ("I", 10, "int32"), ("F", 12, "float32"), ("U", 10, "uint16"), ("X", 10, "bfloat16"), ("G", 16, "bfloat16"),
+        ("E", 16, "bfloat16"), ("D", 16, "bfloat16"), ("AA", 16, "bfloat16"), ("AB", 16, "bfloat16"),
+        ("SO", 32, "bfloat16"),
+    ]:
+        SCRATCH["%s%d" % (_nm, _h)] = ("sbuf", [128, _cols * n], _dt)
+    for _nm in ("PA", "PB", "PS", "PV"):
+        SCRATCH["%s%d" % (_nm, _h)] = ("psum", [128, 512], "float32")
+INPUTS = ("gn", "ar", "mh", "wt", "hk", "th", "y")
+
+
+def v(name, lo, hi, step=1):
+    return (name, lo, hi, step)
+
+
+def cols(d):
+    if d[3] in (1, -1):
+        return ((1 << (d[2] - d[1])) - 1) << d[1]
+    return sum(1 << c for c in range(d[1], d[2], d[3]))
+
+
+def count(d):
+    return len(range(d[1], d[2], abs(d[3])))
+
+
+def ap(T, d):
+    t = T[d[0]]
+    if d[3] == -1:
+        return t[:, d[2] - 1:d[1] - 1:-1]
+    return t[:, d[1]:d[2]] if d[3] == 1 else t[:, d[1]:d[2]:d[3]]
+
+
+def arg(T, x):
+    if not isinstance(x, tuple):
+        return x
+    return ap(T, x[1]).indirect(ap(T, x[2])) if x[0] == "ind" else ap(T, x)
+
+
+def ind(win, off):
+    return ("ind", win, off)
+
+
+def where(d):
+    return SCRATCH[d[0]][0] if d[0] in SCRATCH else "hbm"
+
+
+CY = 1.0
+PCY = 0.6
+GCY = 1.56
+OPS = []
+TAG = [None]
+ARR = {}
+
+
+def add(alts, reads, writes, kind="c", sem=None, after=()):
+    OPS.append({"alt": alts, "eng": sorted(alts)[0] if len(alts) == 1 else "F", "r": reads, "w": writes,
+                "cost": min(x[1] for x in alts.values()), "kind": kind, "sem": sem, "after": list(after),
+                "id": len(OPS), "tag": TAG[0]})
+    return len(OPS) - 1
+
+
+def vcost(out, ins, both=False):
+    if out[0] == "ind":
+        return 50 + 3.8 * CY * count(ins[0])
+    if ins and ins[0][0] == "ind":
+        return 50 + GCY * CY * count(out)
+    if both:
+        c = 2.0 if all(where(x) == "sbuf" for x in ins) else 1.0
+    else:
+        c = 0.5 if all(SCRATCH[x[0]][2] in ("bfloat16", "uint16") for x in ins + [out]) else 1.0
+    return max(64.0, c * count(out)) * CY
+
+
+def rw(out, ins):
+    r = []
+    for x in ins:
+        if isinstance(x, tuple):
+            r += [x[1], x[2]] if x[0] == "ind" else [x]
+    if out[0] == "ind":
+        return r + [out[2]], [out[1]]
+    return r, [out]
+
+
+def v_copy(out, in_):
+    return (lambda c: c["g"].vector.tensor_copy(arg(c["T"], out), arg(c["T"], in_)), vcost(out, [in_]))
+
+
+def s_act(out, in_, func, bias=0.0, scale=1.0):
+    cost = 65 + GCY * CY * count(out) if in_[0] == "ind" else max(64.0, count(out)) * CY
+    return (lambda c: c["g"].scalar.activation(arg(c["T"], out), arg(c["T"], in_), func, bias=arg(c["T"], bias),
+                                               scale=scale), cost)
+
+
+def copy(out, in_):
+    return add({"V": v_copy(out, in_)}, *rw(out, [in_]))
+
+
+def move(out, in_):
+    return add({"V": v_copy(out, in_), "S": s_act(out, in_, ACT.Identity)}, *rw(out, [in_]))
+
+
+def act(out, in_, func, bias=0.0, scale=1.0):
+    return add({"S": s_act(out, in_, func, bias, scale)}, *rw(out, [in_, bias]))
+
+
+def tt(out, a, b, op):
+    return add({"V": (lambda c: c["g"].vector.tensor_tensor(arg(c["T"], out), arg(c["T"], a), arg(c["T"], b), op),
+                      vcost(out, [a, b], True))}, *rw(out, [a, b]))
+
+
+def ts(out, a, s1, op0, s2=None, op1=None):
+    def fn(c):
+        T = c["T"]
+        if op1 is None:
+            return c["g"].vector.tensor_scalar(arg(T, out), arg(T, a), arg(T, s1), None, op0)
+        return c["g"].vector.tensor_scalar(arg(T, out), arg(T, a), arg(T, s1), arg(T, s2), op0, op1)
+    return add({"V": (fn, vcost(out, [a]))}, *rw(out, [a, s1, s2]))
+
+
+def memset(out, val):
+    return add({"V": (lambda c: c["g"].vector.memset(arg(c["T"], out), val), vcost(out, []))}, [], [out])
+
+
+def scan(out, mask, data):
+    return add({"V": (lambda c: c["g"].vector.tensor_tensor_scan(arg(c["T"], out), arg(c["T"], mask),
+                                                                 arg(c["T"], data), 0.0, ALU.mult, ALU.max),
+                      vcost(out, [mask, data]))}, [mask, data], [out])
+
+
+def vtr(out, in_):
+    return add({"V": (lambda c: c["g"].vector.transpose(arg(c["T"], out), arg(c["T"], in_)), vcost(out, [in_]))},
+               [in_], [out])
+
+
+def mm(items, start=True, stop=True):
+    def fn(c):
+        T = c["T"]
+        last = None
+        for i, (o, l, x) in enumerate(items):
+            last = c["g"].tensor.matmul(arg(T, o), arg(T, l), arg(T, x), start and i == 0,
+                                        stop and i == len(items) - 1)
+        return last
+    return add({"P": (fn, sum(max(64, count(x)) for o, l, x in items) * PCY)},
+               [l for o, l, x in items] + [x for o, l, x in items], [o for o, l, x in items])
+
+
+def iota(out, pattern, base, cm):
+    def fn(c):
+        if SCRATCH[out[0]][2] == "int32":
+            return c["g"].iota(arg(c["T"], out), pattern, base, cm)
+        return c["g"].iota(arg(c["T"], out), pattern, base, cm, allow_small_or_imprecise_dtypes=True)
+    return add({"G": (fn, 130 + 2 * CY * count(out))}, [], [out])
+
+
+def asel(out, in_, pattern, op, base, cm):
+    return add({"G": (lambda c: c["g"].affine_select(arg(c["T"], out), arg(c["T"], in_), pattern, op, 0.0, base, cm),
+                      170 + 2 * CY * count(out))}, [in_], [out])
+
+
+def dma(eng, out, in_, nbytes):
+    sem = "d%d" % len(SEMAPHORES)
+    SEMAPHORES.append(sem)
+
+    def fn(c):
+        q = c["g"].sync if eng == "Y" else c["g"].scalar
+        return q.dma_start(arg(c["T"], out), arg(c["T"], in_))
+    return add({eng: (fn, nbytes)}, [] if in_[0] in INPUTS else [in_], [] if out[0] in INPUTS else [out], "d", sem)
+
+
+def share(c, backs):
+    topo, me = c["topo"], c["core"]
+    dsts = [c["T"].cores[(c["rank"] - b) % NR] for b in backs]
+    used = {}
+    out = {}
+    order = sorted(range(len(dsts)), key=lambda i: len(topo.engines(me, dsts[i])))
+    narrow = [i for i in order if len(topo.engines(me, dsts[i])) == len(topo.engines(me, dsts[order[0]]))]
+    for i in order:
+        left = [e for e in topo.engines(me, dsts[i]) if e not in used]
+        k = len(left) // len([j for j in narrow if j not in out]) if i in narrow else len(left)
+        p = 1
+        while 2 * p <= k:
+            p *= 2
+        m = 0
+        for e in left[:p]:
+            used[e] = 1
+            m |= 1 << e
+        out[i] = (dsts[i], m, p)
+    return [out[i] for i in range(len(dsts))]
+
+
+def send(src, dests, nbytes, after=()):
+    backs = [b for b, d, s in dests]
+
+    def fn(c):
+        T, topo = c["T"], c["topo"]
+        trs = []
+        for (core, m, p), (b, d, s) in zip(share(c, backs), dests):
+            assert topo.may_write(c["core"], core)
+            rid, pid, se = topo.addr(core)
+            trs.append(RemoteDMATransfer(dst_ids=[DstId(rid=rid, pnc=pid)], dma_engine_mask=m, remote_sem=T.sem[s],
+                                         src=arg(T, src), dst=arg(T, d)))
+            c["sent"][0] += p
+        c["g"].remote_dma_fused(trs, local_sem=T.sem.sent)
+        return None
+    return add({"G": (fn, nbytes)}, [src], [], "r", after=after)
+
+
+def arrive(sem, writes, calls, sends):
+    SEMAPHORES.append(sem)
+    ARR[sem] = calls
+    return add({"X": (None, 0)}, [], writes, "x", sem, after=sends)
+
+
+def arrival_count(c, sem):
+    tot = 0
+    for back, backs in ARR[sem]:
+        r = (c["rank"] + back) % NR
+        other = {"topo": c["topo"], "T": c["T"], "rank": r, "core": c["T"].cores[r]}
+        tot += share(other, backs)[backs.index(back)][2]
+    return tot
+
+
+def col(name, j):
+    return v(name, j, j + 1)
+
+
+RHO, MCOL, CMC, E0, E1, R32, TCOL, TMPC, CA, CX, R1 = [col("cf", j) for j in range(11)]
+IDN, NIDN, BK, BKN, WB, TB = [v(x, 0, 128) for x in ("idn", "nidn", "bk", "bkn", "wb", "tb")]
+
+
+def phase(t, h):
+    s = (2 * h + 3 * t) % 8
+    return 66 * (s % 4) + 2 * (s // 4)
+
+
+def setup():
+    dma("S", v("wtb", 0, 2), v("wt", 0, 2), 512)
+    dma("S", v("hki", 0, 2), v("hk", 0, 2), 1024)
+    dma("S", v("thi", 0, 2), v("th", 0, 2), 1024)
+    dma("Y", v("W", XOFF, AOFF), v("gn", 0, 4096), 1 << 20)
+    dma("Y", v("W", AOFF, AOFF + 4096), v("ar", 0, 4096), 1 << 20)
+    dma("Y", v("W", PAD, WEND), v("ar", 0, 32), 1 << 13)
+    dma("Y", v("Mo", 0, 2048), v("mh", 0, 2048), 1 << 19)
+    memset(v("ones", 0, 128), 1.0)
+    iota(v("ci", 0, 1), [[0, 1]], 0, 1)
+    iota(v("ci", 8, 32), [[2, 2], [3, 3], [0, 4]], 0, 0)
+    iota(v("ci", 32, 56), [[64, 2], [0, 3], [1024, 4]], 0, 0)
+    iota(v("ci", 56, 80), [[0, 6], [512, 4]], 0, 0)
+    asel(v("blk0", 0, 128), v("ones", 0, 128), [[-16, 8], [0, 16]], ALU.is_ge, 0, 1)
+    asel(v("blk", 0, 128), v("blk0", 0, 128), [[16, 8], [0, 16]], ALU.is_ge, 15, -1)
+    asel(IDN, v("ones", 0, 128), [[-1, 128]], ALU.is_equal, 0, 1)
+    iota(v("ai", 0, 264), [[1, 4], [4, 33], [1, 2]], 0, 0)
+    iota(v("c32", 0, 128), [[64, 2], [128, 32], [32, 2]], 0, 0)
+    iota(v("c32b", 0, 128), [[32, 128]], 0, 0)
+    iota(v("q16", 0, 8), [[2, 2], [32, 4]], 0, 0)
+    ts(v("ci", 1, 2), v("ci", 0, 1), 15, ALU.bitwise_and)
+    copy(RHO, v("ci", 1, 2))
+    ts(R32, RHO, 32.0, ALU.mult)
+    ts(v("ci", 4, 5), v("ci", 0, 1), 1, ALU.bitwise_and)
+    ts(R1, v("ci", 4, 5), -1.0, ALU.mult)
+    ts(CA, RHO, 2.0, ALU.mult, R1, ALU.add)
+    ts(CX, CA, 32.0, ALU.mult)
+    ts(v("ci", 8, 32), v("ci", 8, 32), CA, ALU.add)
+    ts(v("ci", 8, 32), v("ci", 8, 32), 7, ALU.bitwise_and)
+    tt(v("ci", 32, 56), v("ci", 32, 56), v("ci", 8, 32), ALU.add)
+    ts(v("xoff", 0, 24), v("ci", 32, 56), CX, ALU.add)
+    tt(v("ci", 56, 80), v("ci", 56, 80), v("ci", 8, 32), ALU.add)
+    ts(v("xoff", 24, 48), v("ci", 56, 80), R32, ALU.add)
+    ts(v("ai", 0, 264), v("ai", 0, 264), 7, ALU.bitwise_and)
+    copy(v("af", 0, 264), v("ai", 0, 264))
+    copy(v("PF", 0, 2), v("hki", 0, 2))
+    copy(v("PF", 2, 4), v("thi", 0, 2))
+    copy(v("PF", 4, 6), v("wtb", 0, 2))
+    s0 = send(v("PF", 0, 6), [(t + 1, v("PR%d" % t, 0, 6), "ap%d" % t) for t in range(RO)], 3072)
+    s = s0
+    for t in range(RO):
+        s = send(v("Mo", 0, 2048), [(t + 1, v("M%d" % t, 0, 2048), "am%d" % t)], 1 << 19, after=[s])
+        arrive("ap%d" % t, [v("PR%d" % t, 0, 6)], [(t + 1, [1, 2, 3])], [s0])
+        arrive("am%d" % t, [v("M%d" % t, 0, 2048)], [(t + 1, [t + 1])], [s])
+    ts(WB, v("blk", 0, 128), col("PF", 4), ALU.mult)
+    ts(MCOL, RHO, 2.0, ALU.mult, 1.0, ALU.add)
+    ts(CMC, RHO, -32768.0, ALU.mult, 16 * 32768.0 + 4096.0, ALU.add)
+    ts(NIDN, IDN, -1.0, ALU.mult)
+    memset(v("zs", 0, 144), 0.0)
+    ts(v("zs", 15, 128, 16), v("blk", 0, 128, 16), -ES, ALU.mult)
+    ts(E0, RHO, 0.0, ALU.is_equal, ES, ALU.mult)
+    ts(E1, RHO, 1.0, ALU.is_equal, ES, ALU.mult)
+    ts(v("ci", 2, 3), v("thi", 0, 1), 8128, ALU.bitwise_and)
+    ts(v("ci", 3, 4), v("thi", 0, 1), 63, ALU.bitwise_and)
+    ts(TMPC, v("ci", 2, 3), E0, ALU.mult)
+    ts(TCOL, v("ci", 3, 4), E1, ALU.mult, TMPC, ALU.add)
+    ts(TB, v("blk", 0, 128), TCOL, ALU.mult)
+    for q in range(2):
+        j = v("jt", 264 * q, 264 * q + 264)
+        ts(j, v("af", 0, 264), -1.0, ALU.mult, RHO, ALU.add)
+        th = v("PV%d" % q, 0, 264)
+        if q == 0:
+            ts(th, j, 0.0, ALU.is_le, 3.0e7, ALU.mult)
+            ts(j, j, -3.0, ALU.add, 0.0, ALU.max)
+            ts(j, j, float(2 ** 19), ALU.mult, 32768.0, ALU.add)
+            tt(th, j, th, ALU.add)
+        else:
+            ts(th, j, float(2 ** 19), ALU.mult, 13.0 * 2 ** 19 + 32768.0, ALU.add)
+    memset(v("m16", 0, 64), 1.0)
+    memset(v("m16", 0, 64, 16), 0.0)
+    memset(v("m32", 0, 1024), 1.0)
+    memset(v("m32", 0, 1024, 32), 0.0)
+    ts(BK, v("blk", 0, 128), BIG, ALU.mult)
+    ts(BKN, v("blk", 0, 128), -BIG, ALU.mult)
+    ts(v("c32p", 0, 128), v("c32", 0, 128), 4096.0, ALU.add)
+    for t in range(RO):
+        memset(v("cst", 64 * t, 64 * t + 64), -4096.0 * (t + 1))
+        ts(v("wj", 128 * t, 128 * t + 128), v("blk", 0, 128), col("PR%d" % t, 5), ALU.mult)
+    for t in range(RO - 1):
+        ts(v("zw", 144 * t, 144 * t + 144), v("zs", 0, 144), col("PR%d" % t, 5), ALU.mult, -1.0 / ES, ALU.mult)
+
+
+def slot(name, h, k, w=1):
+    return v("%s%d" % (name, h), n * k, n * (k + w))
+
+
+def pv(h, k):
+    return v("PV%d" % h, 320 + n * k, 320 + n * (k + 1))
+
+
+def hash16(h, si, kcol, bound, out16):
+    u, uu, p = slot("I", h, 1), slot("I", h, 2), slot("I", h, 3)
+    ts(u, si, 4095, ALU.bitwise_and)
+    tt(uu, u, u, ALU.mult)
+    ts(pv(h, 0), u, kcol, ALU.mult)
+    ts(uu, uu, 5, ALU.arith_shift_right)
+    tt(uu, uu, pv(h, 0), ALU.add)
+    ts(p, uu, bound - 1, ALU.bitwise_and)
+    copy(out16, p)
+
+
+def diffs(h, y, src, dst):
+    for b, bank in enumerate(("PA", "PB")):
+        reg = [v("%s%d" % (bank, h), n * k, n * (k + 1)) for k in range(8)]
+        gs = [v(src, 8 * b + k, 16 * n, 16) for k in range(8)]
+        if SPLIT_D:
+            mm([(reg[k], NIDN, y) for k in range(8)], True, False)
+            mm([(reg[k], IDN, gs[k]) for k in range(8)], False, True)
+        else:
+            for k in range(8):
+                mm([(reg[k], NIDN, y), (reg[k], IDN, gs[k])])
+        act(v(dst, 512 * b, 512 * b + 512), v("%s%d" % (bank, h), 0, 512), ACT.Abs)
+
+
+def zsel(name, base, m):
+    return v(name, base + 15 - m, base + 143 - m)
+
+
+def flanks(t, h):
+    w0 = XOFF - 4096 * t
+    awin = v("W", AOFF, WEND)
+    xa = slot("X", h, 0) if t == 0 else slot("X", h, 2 + t)
+    beta = v("c32", n * h, n * h + n) if t == 0 else slot("F", h, 0)
+    ps = "PS%d" % h
+    si, u, p, lq = slot("I", h, 0), slot("I", h, 1), slot("I", h, 3), slot("I", h, 4)
+    ba = pv(h, 1)
+    sh = phase(t, h)
+    if t == 0:
+        move(slot("X", h, 0, 3), ind(v("W", XOFF, AOFF), v("xoff", 12 * h, 12 * h + 12)))
+        mm([(v(ps, 0, n), WB, xa)])
+        copy(si, v(ps, 0, n))
+    else:
+        tt(si, v(ps, 0, n), slot("F", h, 1), ALU.min)
+    tt(ba, beta, v("af", sh, sh + n), ALU.add)
+    hash16(h, si, col("PF", 0), 4096, slot("U", h, 0))
+    xo, key = slot("F", h, 2), slot("F", h, 5)
+    ts(lq, u, MCOL, ALU.mult)
+    ts(lq, lq, 4, ALU.arith_shift_right, 15, ALU.bitwise_and)
+    tt(xo, lq, ba, ALU.add)
+    ts(slot("U", h, 2), xo, 4.0 + 4096 * t, ALU.add)
+    tt(pv(h, 2), p, ba, ALU.subtract)
+    tt(slot("F", h, 3), xo, pv(h, 2), ALU.add)
+    ts(slot("U", h, 1), slot("F", h, 3), 4.0, ALU.add)
+    ts(slot("F", h, 4), lq, float(2 ** 19), ALU.mult, CMC, ALU.add)
+    tt(key, slot("F", h, 4), pv(h, 2), ALU.add)
+    if t < RO - 1:
+        xn = slot("X", h, 1) if t == 0 else slot("X", h, 5)
+        mm([(v(ps, n, 2 * n), WB, xn)])
+        act(slot("F", h, 1), v(ps, n, 2 * n), ACT.Identity, bias=float(2 ** 21))
+    G, E, D, AA, AB, U = ["%s%d" % (x, h) for x in ("G", "E", "D", "AA", "AB", "U")]
+    for k in range(2):
+        move(v(G, 512 * k, 512 * k + 512), ind(awin, v(U, 32 * k, 32 * k + 32)))
+    for k in range(2):
+        move(v(E, 512 * k, 512 * k + 512), ind(v("W", w0, AOFF), v(U, 2 * n + 32 * k, 2 * n + 32 * k + 32)))
+    diffs(h, xa, G, AA)
+    e1, e2 = v(ps, 2 * n, 3 * n), v(ps, 3 * n, 4 * n)
+    mm([(e1, TB, v("ones", 0, n))] + [(e1, zsel("zs", 0, m), v(AA, n * m, n * m + n)) for m in range(8)], True, False)
+    mm([(e1, zsel("zs", 0, m), v(AA, n * m, n * m + n)) for m in range(8, 16)], False, True)
+    tt(slot("F", h, 4), key, e1, ALU.min)
+    for k in range(2):
+        tt(v(D, 512 * k, 512 * k + 512), ind(awin, v(U, n + 32 * k, n + 32 * k + 32)), v(E, 512 * k, 512 * k + 512),
+           ALU.subtract)
+        act(v(AB, 512 * k, 512 * k + 512), v(D, 512 * k, 512 * k + 512), ACT.Abs)
+    mm([(e2, TB, v("ones", 0, n))] + [(e2, zsel("zs", 0, m), v(AB, m, 16 * n, 16)) for m in range(16)])
+    k2, tr, s1 = slot("F", h, 5), slot("F", h, 6), slot("F", h, 7)
+    tt(k2, slot("F", h, 4), e2, ALU.min)
+    vtr(tr, k2)
+    scan(s1, v("m16", 0, n), tr)
+    s2, best, dl = slot("I", h, 5), slot("I", h, 6), slot("I", h, 7)
+    scan((s2[0], s2[1], s2[2], -1), v("m16", 0, n), (s1[0], s1[1], s1[2], -1))
+    vtr(best, s2)
+    ts(dl, best, 32767, ALU.bitwise_and)
+    for q in range(2):
+        mk = pv(h, 2 * q)
+        tt(mk, best, v("PV%d" % q, sh, sh + n), ALU.is_ge)
+        tt(mk, dl, mk, ALU.mult)
+        tt(slot("F", h, 8 + q), beta, mk, ALU.add)
+        ts(v(U, 4 * n + q, 6 * n, 2), slot("F", h, 8 + q), RHO, ALU.add, 16.0 * q + 4096 * t, ALU.add)
+    t0 = w0 - 4096 + 2048 * h
+    lo = 0
+    for k in CFG["tg"]:
+        move(v("W", t0 + lo, t0 + lo + k), ind(v("W", w0, WEND), v(U, 4 * n + lo // 16, 4 * n + (lo + k) // 16)))
+        scan(v("SO%d" % h, lo, lo + k), v("m32", 0, k), v("W", t0 + lo, t0 + lo + k))
+        lo += k
+
+
+def verdict(t, h):
+    w0 = XOFF - 4096 * t
+    t0 = w0 - 4096 + 2048 * h
+    ps, pa, pb = "PS%d" % h, "PA%d" % h, "PB%d" % h
+    z = v("SO%d" % h, 31, 32 * n, 32)
+    G, AA, U = "G%d" % h, "AA%d" % h, "U%d" % h
+    pr = "PR%d" % t
+    si = slot("I", h, 0)
+    mm([(v(ps, 4 * n, 5 * n), v("wj", 128 * t, 128 * t + 128), z)])
+    copy(si, v(ps, 4 * n, 5 * n))
+    hash16(h, si, col(pr, 1), 2048, slot("U", h, 3))
+    if t < RO - 1:
+        move(slot("X", h, 6, 2 - t), ind(v("W", t0, t0 + 2048), v("xoff", 24 + 12 * h + 4 * t + 4, 36 + 12 * h)))
+        asel(v("zc%d" % t, n * h, n * h + n), z, [[0, n]], ALU.is_ge, 0, 0)
+        if h == NCH - 1:
+            memory_write(t)
+    for k in range(2):
+        move(v(G, 512 * k, 512 * k + 512), ind(v("M%d" % t, 0, 2048), v(U, 3 * n + 32 * k, 3 * n + 32 * k + 32)))
+    diffs(h, z, G, AA)
+    dm = v(ps, 5 * n, 6 * n)
+    mm([(dm, zsel("zs", 0, m), v(AA, n * m, n * m + n)) for m in range(8)], True, False)
+    mm([(dm, zsel("zs", 0, m), v(AA, n * m, n * m + n)) for m in range(8, 16)], False, True)
+    hit = slot("X", h, 8)
+    act(hit, dm, ACT.Relu, bias=col(pr, 3), scale=1.0 / ES)
+    cb = v(pa, 0, n)
+    if t < RO - 1:
+        mm([(v(ps, 0, n), WB, slot("X", h, 6)), (v(ps, 0, n), BK, hit)])
+    mm([(cb, IDN, v("c32b", n * h, n * h + n)), (cb, IDN, v("cst", 64 * t, 64 * t + n)), (cb, BK, hit)])
+    beta = v("c32", n * h, n * h + n) if t == 0 else slot("F", h, 0)
+    if t < RO - 1 and h == 0:
+        ta = v("F0", 10 * n, 10 * n + 32)
+        tt(ta, v(pa, t, n, 2), v("c32p", t, n, 2), ALU.min)
+        for q in range(2):
+            ts(v(U, 6 * n + q, 7 * n, 2), ta, RHO, ALU.add, 16.0 * q + 4096 * (t + 1), ALU.add)
+        for k in range(2):
+            move(v("tmp", 512 * k, 512 * k + 512), ind(v("W", w0 - 4096, WEND), v(U, 6 * n + 32 * k, 6 * n + 32 * k + 32)))
+    tt(slot("F", h, 0), beta, cb, ALU.min)
+    if t < RO - 1:
+        for b, lo in ((BK, 0), (BKN, 2 * n)):
+            for j in range(2 - t):
+                reg = v(pb, lo + n * j, lo + n * j + n)
+                mm([(reg, IDN, slot("X", h, 6 + j)), (reg, b, hit)])
+        pairs = [(3, 1), (5, 2)] if t == 0 else [(4, 5)]
+        for j, (new, old) in enumerate(pairs):
+            tt(slot("X", h, new), slot("X", h, old), v(pb, n * j, n * j + n), ALU.min)
+            tt(slot("X", h, new), slot("X", h, new), v(pb, 2 * n + n * j, 3 * n + n * j), ALU.max)
+    else:
+        for j in range(2):
+            for q in range(2):
+                ts(v("yo", 4 * h + 2 * j + q, 256, 8), v("F%d" % h, j, n, 2), RHO, ALU.add,
+                   16.0 * q + 4096 * RO, ALU.add)
+        if h == NCH - 1:
+            for lo in range(0, 4096, 512):
+                move(v("Y", lo, lo + 512), ind(v("W", 0, AOFF), v("yo", lo // 16, lo // 16 + 32)))
+                if lo % 1024:
+                    dma("Y", v("y", lo - 512, lo + 512), v("Y", lo - 512, lo + 512), 256 * 1024)
+
+
+def memory_write(t):
+    zc, so = "zc%d" % t, "so%d" % t
+    sc = v("PS1", 6 * n, 6 * n + 8)
+    mm([(sc, zsel("zw", 144 * t, r), v(zc, r, 128, 16)) for r in range(16)])
+    copy(v("si", 0, 8), sc)
+    ts(v("si", 8, 16), v("si", 0, 8), 15, ALU.bitwise_and)
+    ts(v("sf", 0, 8), v("si", 8, 16), 128.0, ALU.mult, CA, ALU.add)
+    tt(v("sf", 8, 16), v("sf", 0, 8), v("q16", 0, 8), ALU.add)
+    copy(v(so, 0, 8), v("sf", 8, 16))
+    lands = [(1, 0), (2, 1)] if t == 0 else [(1, 2)]
+    backs = [b for b, k in lands]
+    a = send(v(zc, 0, 128), [(b, v("zl%d" % k, 0, 128), "az%d" % k) for b, k in lands], 32768)
+    b2 = send(v(so, 0, 8), [(b, v("sl%d" % k, 0, 8), "az%d" % k) for b, k in lands], 2048)
+    for b, k in lands:
+        arrive("az%d" % k, [v("zl%d" % k, 0, 128), v("sl%d" % k, 0, 8)], [(b, backs), (b, backs)], [a, b2])
+        copy(ind(v("M%d" % (1 if k == 0 else 2), 0, 2048), v("sl%d" % k, 0, 8)), v("zl%d" % k, 0, 128))
+
+
+def archive_write(t):
+    for k in range(32):
+        a0 = AOFF + 128 * k + 32 * t
+        move(v("W", a0, a0 + 32), v("tmp", 32 * k, 32 * k + 32))
+    if t == 0:
+        move(v("W", PAD, PAD + 32), v("tmp", 0, 32))
+
+
+def build():
+    setup()
+    for t in range(RO):
+        for h in range(NCH):
+            TAG[0] = (t, h)
+            flanks(t, h)
+        for h in range(NCH):
+            TAG[0] = (t, h)
+            verdict(t, h)
+        if t < RO - 1:
+            TAG[0] = (t, 0)
+            archive_write(t)
+    seen = {}
+    for o in OPS:
+        dep = dict((d, False) for d in o["after"])
+        acc = [(x, cols(x), False) for x in o["r"]] + [(x, cols(x), True) for x in o["w"]]
+        for x, m, wr in acc:
+            ps = where(x) == "psum"
+            for (j, mj, wj) in seen.get(x[0], []):
+                e = OPS[j]["eng"]
+                if ps and e == "P" and o["eng"] == "P":
+                    dep.setdefault(j, False)
+                elif (ps and e != o["eng"]) or ((wr or wj) and (m & mj)):
+                    dep[j] = True
+        for x, m, wr in acc:
+            seen.setdefault(x[0], []).append((o["id"], m, wr))
+        o["dep"] = dep
+        o["succ"] = []
+        for d in dep:
+            OPS[d]["succ"].append(o["id"])
+
+
+LAT = {"same": 50.0, "cross": 110.0, "issue": 60.0, "dma": 1800.0, "rate": 200.0, "rem": 2500.0, "rrate": 80.0}
+
+
+def priorities(bias):
+    prio = [0.0] * len(OPS)
+    for o in OPS[::-1]:
+        span = o["cost"]
+        if o["kind"] == "d":
+            span = LAT["dma"] + o["cost"] / LAT["rate"]
+        if o["kind"] == "r":
+            span = 1000.0 + LAT["rem"] + o["cost"] / LAT["rrate"]
+        prio[o["id"]] = span + LAT["cross"] + max([prio[s] for s in o["succ"]] + [0.0])
+    return [prio[o["id"]] + (bias if o["tag"] is None or o["tag"][1] == 0 else 0.0) for o in OPS]
+
+
+def nudge(prio, seed):
+    s = (seed * 1103515245 + 12345) % (1 << 31)
+    a = (s >> 8) % len(prio)
+    s = (s * 1103515245 + 12345) % (1 << 31)
+    k = (1, 2, 4, 10, 30, 60)[(s >> 8) % 6]
+    s = (s * 1103515245 + 12345) % (1 << 31)
+    d = ((s >> 8) % 2001 - 1000) * 3.0
+    return prio[:a] + [x + d for x in prio[a:a + k]] + prio[a + k:]
+
+
+def schedule(prio, delta, pen):
+    N = len(OPS)
+    left = [len(o["dep"]) for o in OPS]
+    ready = [dict((e, 0.0) for e in o["alt"]) for o in OPS]
+    fin = [0.0] * N
+    beg = [0.0] * N
+    free = dict((e, 0.0) for e in "VSPGYX")
+    dma_free = [0.0, 0.0]
+    cand = [i for i in range(N) if left[i] == 0]
+    order = dict((e, []) for e in "VSPGYX")
+    while cand:
+        t0, e = min((max(r, free[q]), q) for i in cand for q, r in ready[i].items())
+        lim = t0 + delta
+        able = [i for i in cand if ready[i].get(e, 1e18) <= lim]
+        if e == "Y":
+            pick = min(able)
+        else:
+            pick = max(able, key=lambda i: (prio[i] - (pen if e == "V" and OPS[i]["eng"] == "F" else 0.0), -i))
+        o = OPS[pick]
+        t = max(ready[pick][e], free[e])
+        cost = o["alt"][e][1]
+        beg[pick] = t
+        if o["kind"] == "d":
+            free[e] = t + LAT["issue"]
+            if e == "Y":
+                dma_free[0] = max(dma_free[0], free[e]) + cost / LAT["rate"]
+            fin[pick] = (dma_free[0] if e == "Y" else t) + LAT["dma"]
+        elif o["kind"] == "r":
+            free[e] = t + 1000.0
+            dma_free[1] = max(dma_free[1], free[e]) + cost / LAT["rrate"]
+            fin[pick] = dma_free[1] + LAT["rem"]
+        elif o["kind"] == "x":
+            fin[pick] = t
+        else:
+            free[e] = t + cost
+            fin[pick] = free[e]
+        order[e].append(pick)
+        cand.remove(pick)
+        for j in o["succ"]:
+            r = ready[j]
+            for q in r:
+                if o["kind"] == "r" and OPS[j]["kind"] == "r":
+                    at = free[e]
+                elif not OPS[j]["dep"][pick]:
+                    at = fin[pick]
+                else:
+                    at = fin[pick] + (LAT["same"] if q == e else LAT["cross"])
+                if at > r[q]:
+                    r[q] = at
+            left[j] -= 1
+            if left[j] == 0:
+                cand.append(j)
+    return max(fin), order, beg, fin
+
+
+def plan():
+    prio = priorities(CFG["bias"])
+    for s in CFG["steps"]:
+        prio = nudge(prio, s)
+    return schedule(prio, CFG["delta"], CFG["pen"])
+
+
+build()
+PLAN = [plan()]
+
+
+def rank_program(g, core, T, topo):
+    rank = T.rank_of(core)
+    if rank is None:
+        return
+    c = {"g": g, "T": T, "topo": topo, "rank": rank, "core": core, "sent": [0]}
+    order = PLAN[0][1]
+    queue = {"V": g.vector, "S": g.scalar, "P": g.tensor, "G": g, "Y": g.sync}
+    mark = {}
+    total = {}
+    for e in "VSPG":
+        k = 0
+        for i in order[e]:
+            if OPS[i]["kind"] == "c":
+                k += 1
+                mark[i] = ("c" + e, k)
+        total["c" + e] = k
+    for o in OPS:
+        if o["kind"] in "dx":
+            mark[o["id"]] = (o["sem"], 16 if o["kind"] == "d" else arrival_count(c, o["sem"]))
+            total[o["sem"]] = mark[o["id"]][1]
+    done = {}
+    for e in "YSGPV":
+        q = queue[e]
+        seen = {}
+        for i in order[e]:
+            o = OPS[i]
+            need = {}
+            for d, real in o["dep"].items():
+                if real and d in mark:
+                    s, k = mark[d]
+                    need[s] = max(need.get(s, 0), k)
+            for s, k in sorted(need.items()):
+                if seen.get(s, 0) < k:
+                    q.wait_ge(T.sem[s], k)
+                    seen[s] = k
+                    done[s] = max(done.get(s, 0), k)
+            ins = o["alt"][e][0](c)
+            if o["kind"] == "c":
+                ins.then_inc(T.sem["c" + e], 1)
+            elif o["kind"] == "d":
+                ins.then_inc(T.sem[o["sem"]], 16)
+    total["sent"] = c["sent"][0]
+    for s, k in sorted(total.items()):
+        if done.get(s, 0) < k:
+            g.sync.wait_ge(T.sem[s], k)

@@ -8,13 +8,13 @@ NR = 4
 RO = 3
 n = 64
 NCH = 2
-SPLIT_D = True
 XOFF, AOFF, PAD, WEND = 12288, 16384, 20480, 20512
 BIG = float(2 ** 22)
 ES = float(2 ** 25)
 
-CFG = {"tg": [512, 512, 512, 512], "delta": 60.0, "bias": 1000.0, "pen": 3000.0,
-       "steps": [5, 10, 12, 47, 52, 53, 78, 104, 114, 117, 131, 139, 200, 206, 216, 218, 316, 358, 425, 490, 511, 538]}
+CFG = {"tg": [512, 512, 512, 512], "delta": 100.0, "bias": 6000.0, "pen": 6000.0,
+       "steps": [5, 23, 25, 27, 45, 53, 62, 87, 267, 270, 422, 438, 457, 493, 506, 613, 878, 915, 947, 1028]}
+LAT = {"same": 180.0, "cross": 250.0, "issue": 60.0, "dma": 1800.0, "rate": 200.0, "rem": 4000.0, "rrate": 50.0}
 
 SCRATCH = {}
 SEMAPHORES = ["cV", "cS", "cP", "cG", "sent"]
@@ -271,9 +271,9 @@ def setup():
     dma("S", v("hki", 0, 2), v("hk", 0, 2), 1024)
     dma("S", v("thi", 0, 2), v("th", 0, 2), 1024)
     dma("Y", v("W", XOFF, AOFF), v("gn", 0, 4096), 1 << 20)
+    dma("Y", v("Mo", 0, 2048), v("mh", 0, 2048), 1 << 19)
     dma("Y", v("W", AOFF, AOFF + 4096), v("ar", 0, 4096), 1 << 20)
     dma("Y", v("W", PAD, WEND), v("ar", 0, 32), 1 << 13)
-    dma("Y", v("Mo", 0, 2048), v("mh", 0, 2048), 1 << 19)
     memset(v("ones", 0, 128), 1.0)
     iota(v("ci", 0, 1), [[0, 1]], 0, 1)
     iota(v("ci", 8, 32), [[2, 2], [3, 3], [0, 4]], 0, 0)
@@ -304,12 +304,14 @@ def setup():
     copy(v("PF", 0, 2), v("hki", 0, 2))
     copy(v("PF", 2, 4), v("thi", 0, 2))
     copy(v("PF", 4, 6), v("wtb", 0, 2))
-    s0 = send(v("PF", 0, 6), [(t + 1, v("PR%d" % t, 0, 6), "ap%d" % t) for t in range(RO)], 3072)
+    s0 = send(v("PF", 0, 6), [(t + 1, v("PR%d" % t, 0, 6), "ap%d" % t) for t in range(RO)], 3072,
+              after=[o["id"] for o in OPS if o["eng"] == "G"])
     s = s0
-    for t in range(RO):
+    for t in range(RO - 1):
         s = send(v("Mo", 0, 2048), [(t + 1, v("M%d" % t, 0, 2048), "am%d" % t)], 1 << 19, after=[s])
         arrive("ap%d" % t, [v("PR%d" % t, 0, 6)], [(t + 1, [1, 2, 3])], [s0])
         arrive("am%d" % t, [v("M%d" % t, 0, 2048)], [(t + 1, [t + 1])], [s])
+    arrive("ap2", [v("PR2", 0, 6)], [(3, [1, 2, 3])], [s0])
     ts(WB, v("blk", 0, 128), col("PF", 4), ALU.mult)
     ts(MCOL, RHO, 2.0, ALU.mult, 1.0, ALU.add)
     ts(CMC, RHO, -32768.0, ALU.mult, 16 * 32768.0 + 4096.0, ALU.add)
@@ -371,12 +373,8 @@ def diffs(h, y, src, dst):
     for b, bank in enumerate(("PA", "PB")):
         reg = [v("%s%d" % (bank, h), n * k, n * (k + 1)) for k in range(8)]
         gs = [v(src, 8 * b + k, 16 * n, 16) for k in range(8)]
-        if SPLIT_D:
-            mm([(reg[k], NIDN, y) for k in range(8)], True, False)
-            mm([(reg[k], IDN, gs[k]) for k in range(8)], False, True)
-        else:
-            for k in range(8):
-                mm([(reg[k], NIDN, y), (reg[k], IDN, gs[k])])
+        mm([(reg[k], NIDN, y) for k in range(8)], True, False)
+        mm([(reg[k], IDN, gs[k]) for k in range(8)], False, True)
         act(v(dst, 512 * b, 512 * b + 512), v("%s%d" % (bank, h), 0, 512), ACT.Abs)
 
 
@@ -523,6 +521,9 @@ def memory_write(t):
     backs = [b for b, k in lands]
     a = send(v(zc, 0, 128), [(b, v("zl%d" % k, 0, 128), "az%d" % k) for b, k in lands], 32768)
     b2 = send(v(so, 0, 8), [(b, v("sl%d" % k, 0, 8), "az%d" % k) for b, k in lands], 2048)
+    if t == 0:
+        s = send(v("Mo", 0, 2048), [(3, v("M2", 0, 2048), "am2")], 1 << 19, after=[b2])
+        arrive("am2", [v("M2", 0, 2048)], [(3, [3])], [s])
     for b, k in lands:
         arrive("az%d" % k, [v("zl%d" % k, 0, 128), v("sl%d" % k, 0, 8)], [(b, backs), (b, backs)], [a, b2])
         copy(ind(v("M%d" % (1 if k == 0 else 2), 0, 2048), v("sl%d" % k, 0, 8)), v("zl%d" % k, 0, 128))
@@ -566,9 +567,6 @@ def build():
         o["succ"] = []
         for d in dep:
             OPS[d]["succ"].append(o["id"])
-
-
-LAT = {"same": 50.0, "cross": 110.0, "issue": 60.0, "dma": 1800.0, "rate": 200.0, "rem": 2500.0, "rrate": 80.0}
 
 
 def priorities(bias):

@@ -6,39 +6,48 @@ ACT = ActivationFunctionType
 
 NR = 4
 RO = 3
-n = 64
-NCH = 2
-XOFF, AOFF, PAD, WEND = 12288, 16384, 20480, 20512
+XOFF, AOFF, AS = 12288, 16384, 4128
+WEND = AOFF + RO * AS
 BIG = float(2 ** 22)
 ES = float(2 ** 25)
+KU = 2 ** 18
+FL = 2 ** 23
 
-CFG = {"tg": [512, 512, 512, 512], "delta": 100.0, "bias": 6000.0, "pen": 6000.0,
-       "steps": [5, 23, 25, 27, 45, 53, 62, 87, 267, 270, 422, 438, 457, 493, 506, 613, 878, 915, 947, 1028]}
-LAT = {"same": 180.0, "cross": 250.0, "issue": 60.0, "dma": 1800.0, "rate": 200.0, "rem": 4000.0, "rrate": 50.0}
+CFG = {"chunks": [(0, 2), (2, 2)], "order": [[0, 1], [0, 1], [0, 1]], "piece": 512, "both": False,
+       "arch": "tmp", "gcopy": True, "ypiece": 2, "bias": 2000.0, "delta": 250.0, "pen": 6000.0, "slack": 100.0,
+       "steps": [12, 16, 30, 37, 55, 65, 68, 69, 123, 137, 138, 139, 145, 146, 155, 183, 197, 217, 220, 281, 309, 313, 326, 336, 349, 350, 391, 398, 403, 423, 459, 537, 671, 714, 786, 796, 867, 871, 927, 946, 997, 999, 1006, 1032, 1045, 1057, 1130, 1183, 1367, 1370, 1380, 1442, 1660, 1734, 1837, 1850, 1987, 2375]}
+MODEL = {"cy": 0.9, "g": 1.56, "sc": 3.8, "pcy": 0.5, "same": 220.0, "cross": 240.0, "issue": 60.0, "dma": 1300.0,
+         "rate": 330.0, "riss": 700.0, "rfirst": 2500.0, "rem": 1800.0, "rrate": 70.0}
+
+CH = CFG["chunks"]
+NG = [32 * w for s, w in CH]
+OWN = sum(w + 1 for s, w in CH) < 8
 
 SCRATCH = {}
 SEMAPHORES = ["cV", "cS", "cP", "cG", "sent"]
 for _dt, _list in [
-    ("bfloat16", [("W", WEND), ("Y", 4096), ("Mo", 2048), ("M0", 2048), ("M1", 2048), ("M2", 2048), ("wtb", 8),
+    ("bfloat16", [("W", WEND), ("Mo", 2048), ("M0", 2048), ("M1", 2048), ("M2", 2048), ("wtb", 8),
                   ("ones", 128), ("blk0", 128), ("blk", 128), ("idn", 128), ("nidn", 128), ("bk", 128), ("bkn", 128),
-                  ("wb", 128), ("tb", 128), ("wj", 384), ("zs", 144), ("zw", 288), ("c32b", 128), ("cst", 192),
+                  ("wb", 128), ("tb", 128), ("wj", 384), ("zs", 144), ("zw", 288), ("c16", 256), ("cst", 512),
                   ("m32", 1024), ("tmp", 1024), ("zc0", 128), ("zc1", 128), ("zl0", 128), ("zl1", 128), ("zl2", 128)]),
-    ("float32", [("PF", 8), ("PR0", 8), ("PR1", 8), ("PR2", 8), ("c32", 128), ("c32p", 128), ("af", 264),
-                 ("jt", 528), ("cf", 16), ("m16", 64), ("q16", 8), ("sf", 16)]),
-    ("int32", [("hki", 4), ("thi", 4), ("ai", 264), ("ci", 80), ("si", 16)]),
-    ("uint16", [("xoff", 48), ("yo", 256), ("so0", 8), ("so1", 8), ("sl0", 8), ("sl1", 8), ("sl2", 8)]),
+    ("float32", [("PF", 8), ("PR0", 8), ("PR1", 8), ("PR2", 8), ("b0", 256), ("ba", 128), ("t0", 288), ("cf", 32),
+                 ("m16", 64), ("q8", 8), ("sf", 8)]),
+    ("int32", [("hki", 4), ("thi", 4), ("ai", 288), ("ci", 8), ("si", 16)]),
+    ("uint16", [("so0", 8), ("so1", 8), ("sl0", 8), ("sl1", 8), ("sl2", 8)]),
 ]:
     for _nm, _cols in _list:
         SCRATCH[_nm] = ("sbuf", [128, _cols], _dt)
-for _h in range(NCH):
+SCRATCH["Y"] = ("sbuf", [128, 16, 256], "bfloat16")
+for _h, _n in enumerate(NG):
     for _nm, _cols, _dt in [
-        ("I", 10, "int32"), ("F", 12, "float32"), ("U", 10, "uint16"), ("X", 10, "bfloat16"), ("G", 16, "bfloat16"),
-        ("E", 16, "bfloat16"), ("D", 16, "bfloat16"), ("AA", 16, "bfloat16"), ("AB", 16, "bfloat16"),
-        ("SO", 32, "bfloat16"),
+        ("I", 7, "int32"), ("F", 18, "float32"), ("U", 10, "uint16"), ("X", 7, "bfloat16"), ("G", 16, "bfloat16"),
+        ("E", 16, "bfloat16"), ("D", 16, "bfloat16"), ("A", 32, "bfloat16"), ("SO", 32, "bfloat16"),
     ]:
-        SCRATCH["%s%d" % (_nm, _h)] = ("sbuf", [128, _cols * n], _dt)
-    for _nm in ("PA", "PB", "PS", "PV"):
+        SCRATCH["%s%d" % (_nm, _h)] = ("sbuf", [128, _cols * _n], _dt)
+    for _nm in ["PS", "PA", "PB"][:1 + CH[_h][1]]:
         SCRATCH["%s%d" % (_nm, _h)] = ("psum", [128, 512], "float32")
+if OWN:
+    SCRATCH["PV"] = ("psum", [128, 512], "float32")
 INPUTS = ("gn", "ar", "mh", "wt", "hk", "th", "y")
 
 
@@ -46,18 +55,33 @@ def v(name, lo, hi, step=1):
     return (name, lo, hi, step)
 
 
+def rows(name, r0, r1, lo, hi):
+    return (name, r0, r1, lo, hi)
+
+
+def sub(d, lo, hi, step=1):
+    return (d[0], d[1] + lo * d[3], min(d[2], d[1] + hi * d[3]), d[3] * step)
+
+
 def cols(d):
+    if len(d) == 5:
+        row = SCRATCH[d[0]][1][2]
+        return sum(((1 << (d[4] - d[3])) - 1) << (row * r + d[3]) for r in range(d[1], d[2]))
     if d[3] in (1, -1):
         return ((1 << (d[2] - d[1])) - 1) << d[1]
     return sum(1 << c for c in range(d[1], d[2], d[3]))
 
 
 def count(d):
+    if len(d) == 5:
+        return (d[2] - d[1]) * (d[4] - d[3])
     return len(range(d[1], d[2], abs(d[3])))
 
 
 def ap(T, d):
     t = T[d[0]]
+    if len(d) == 5:
+        return t[:, d[1]:d[2], d[3]:d[4]]
     if d[3] == -1:
         return t[:, d[2] - 1:d[1] - 1:-1]
     return t[:, d[1]:d[2]] if d[3] == 1 else t[:, d[1]:d[2]:d[3]]
@@ -77,9 +101,6 @@ def where(d):
     return SCRATCH[d[0]][0] if d[0] in SCRATCH else "hbm"
 
 
-CY = 1.0
-PCY = 0.6
-GCY = 1.56
 OPS = []
 TAG = [None]
 ARR = {}
@@ -87,21 +108,20 @@ ARR = {}
 
 def add(alts, reads, writes, kind="c", sem=None, after=()):
     OPS.append({"alt": alts, "eng": sorted(alts)[0] if len(alts) == 1 else "F", "r": reads, "w": writes,
-                "cost": min(x[1] for x in alts.values()), "kind": kind, "sem": sem, "after": list(after),
-                "id": len(OPS), "tag": TAG[0]})
+                "kind": kind, "sem": sem, "after": list(after), "id": len(OPS), "tag": TAG[0]})
     return len(OPS) - 1
 
 
 def vcost(out, ins, both=False):
     if out[0] == "ind":
-        return 50 + 3.8 * CY * count(ins[0])
+        return (50, 0, 0, count(ins[0]), 0)
     if ins and ins[0][0] == "ind":
-        return 50 + GCY * CY * count(out)
+        return (50, 0, count(out), 0, 0)
     if both:
         c = 2.0 if all(where(x) == "sbuf" for x in ins) else 1.0
     else:
         c = 0.5 if all(SCRATCH[x[0]][2] in ("bfloat16", "uint16") for x in ins + [out]) else 1.0
-    return max(64.0, c * count(out)) * CY
+    return (0, max(64.0, c * count(out)), 0, 0, 0)
 
 
 def rw(out, ins):
@@ -119,17 +139,25 @@ def v_copy(out, in_):
 
 
 def s_act(out, in_, func, bias=0.0, scale=1.0):
-    cost = 65 + GCY * CY * count(out) if in_[0] == "ind" else max(64.0, count(out)) * CY
+    cost = (65, 0, count(out), 0, 0) if in_[0] == "ind" else (0, max(64.0, count(out)), 0, 0, 0)
     return (lambda c: c["g"].scalar.activation(arg(c["T"], out), arg(c["T"], in_), func, bias=arg(c["T"], bias),
                                                scale=scale), cost)
+
+
+def g_sel(out, in_, pattern, op, base, cm):
+    return (lambda c: c["g"].affine_select(arg(c["T"], out), arg(c["T"], in_), pattern, op, 0.0, base, cm),
+            (170, 2 * count(out), 0, 0, 0))
 
 
 def copy(out, in_):
     return add({"V": v_copy(out, in_)}, *rw(out, [in_]))
 
 
-def move(out, in_):
-    return add({"V": v_copy(out, in_), "S": s_act(out, in_, ACT.Identity)}, *rw(out, [in_]))
+def move(out, in_, pool=False):
+    alts = {"V": v_copy(out, in_), "S": s_act(out, in_, ACT.Identity)}
+    if pool:
+        alts["G"] = g_sel(out, in_, [[0, count(out)]], ALU.is_ge, 0, 0)
+    return add(alts, *rw(out, [in_]))
 
 
 def act(out, in_, func, bias=0.0, scale=1.0):
@@ -173,7 +201,7 @@ def mm(items, start=True, stop=True):
             last = c["g"].tensor.matmul(arg(T, o), arg(T, l), arg(T, x), start and i == 0,
                                         stop and i == len(items) - 1)
         return last
-    return add({"P": (fn, sum(max(64, count(x)) for o, l, x in items) * PCY)},
+    return add({"P": (fn, (0, 0, 0, 0, sum(max(64, count(x)) for o, l, x in items)))},
                [l for o, l, x in items] + [x for o, l, x in items], [o for o, l, x in items])
 
 
@@ -182,22 +210,24 @@ def iota(out, pattern, base, cm):
         if SCRATCH[out[0]][2] == "int32":
             return c["g"].iota(arg(c["T"], out), pattern, base, cm)
         return c["g"].iota(arg(c["T"], out), pattern, base, cm, allow_small_or_imprecise_dtypes=True)
-    return add({"G": (fn, 130 + 2 * CY * count(out))}, [], [out])
+    return add({"G": (fn, (130, 2 * count(out), 0, 0, 0))}, [], [out])
 
 
 def asel(out, in_, pattern, op, base, cm):
-    return add({"G": (lambda c: c["g"].affine_select(arg(c["T"], out), arg(c["T"], in_), pattern, op, 0.0, base, cm),
-                      170 + 2 * CY * count(out))}, [in_], [out])
+    return add({"G": g_sel(out, in_, pattern, op, base, cm)}, [in_], [out])
 
 
-def dma(eng, out, in_, nbytes):
+def dma(eng, out, in_, after=()):
     sem = "d%d" % len(SEMAPHORES)
     SEMAPHORES.append(sem)
+    side = in_ if out[0] in INPUTS else out
+    nbytes = 128 * count(side) * (2 if SCRATCH[side[0]][2] == "bfloat16" else 4)
 
     def fn(c):
         q = c["g"].sync if eng == "Y" else c["g"].scalar
         return q.dma_start(arg(c["T"], out), arg(c["T"], in_))
-    return add({eng: (fn, nbytes)}, [] if in_[0] in INPUTS else [in_], [] if out[0] in INPUTS else [out], "d", sem)
+    return add({eng: (fn, nbytes)}, [] if in_[0] in INPUTS else [in_], [] if out[0] in INPUTS else [out], "d", sem,
+               after=after)
 
 
 def share(c, backs):
@@ -257,266 +287,316 @@ def col(name, j):
     return v(name, j, j + 1)
 
 
-RHO, MCOL, CMC, E0, E1, R32, TCOL, TMPC, CA, CX, R1 = [col("cf", j) for j in range(11)]
+RHO, MCOL, E0, E1, TCOL, TMPC, Q0, Q1, R8 = [col("cf", j) for j in range(9)]
+CMC = [col("cf", 10 + t) for t in range(RO)]
+KAP = [col("cf", 14 + t) for t in range(RO)]
+KT = [col("cf", 18 + t) for t in range(RO)]
 IDN, NIDN, BK, BKN, WB, TB = [v(x, 0, 128) for x in ("idn", "nidn", "bk", "bkn", "wb", "tb")]
 
 
-def phase(t, h):
-    s = (2 * h + 3 * t) % 8
-    return 66 * (s % 4) + 2 * (s // 4)
+def abase(t):
+    return AOFF + AS * t
+
+
+def tbase(t, h):
+    if t < 0:
+        return XOFF
+    o = CFG["order"][t]
+    return XOFF - 4096 * t - 32 * sum(NG[k] for k in o[:o.index(h) + 1])
+
+
+def place(t, h, blk):
+    return (CH[h][0] + blk // 2 + 4 * (blk % 2) + 3 * t) % 8
+
+
+def gene0(h, blk):
+    return CH[h][0] + blk // 2 + 4 * (blk % 2)
 
 
 def setup():
-    dma("S", v("wtb", 0, 2), v("wt", 0, 2), 512)
-    dma("S", v("hki", 0, 2), v("hk", 0, 2), 1024)
-    dma("S", v("thi", 0, 2), v("th", 0, 2), 1024)
-    dma("Y", v("W", XOFF, AOFF), v("gn", 0, 4096), 1 << 20)
-    dma("Y", v("Mo", 0, 2048), v("mh", 0, 2048), 1 << 19)
-    dma("Y", v("W", AOFF, AOFF + 4096), v("ar", 0, 4096), 1 << 20)
-    dma("Y", v("W", PAD, WEND), v("ar", 0, 32), 1 << 13)
+    dma("S", v("wtb", 0, 2), v("wt", 0, 2))
+    dma("S", v("hki", 0, 2), v("hk", 0, 2))
+    dma("S", v("thi", 0, 2), v("th", 0, 2))
+    dma("Y", v("W", XOFF, AOFF), v("gn", 0, 4096))
+    dma("Y", v("Mo", 0, 2048), v("mh", 0, 2048))
+    dma("Y", v("W", AOFF, AOFF + 4096), v("ar", 0, 4096))
+    dma("Y", v("W", AOFF + 4096, AOFF + AS), v("ar", 0, 32))
+    dma("Y", v("W", abase(1), abase(1) + 4096), v("ar", 0, 4096))
     memset(v("ones", 0, 128), 1.0)
-    iota(v("ci", 0, 1), [[0, 1]], 0, 1)
-    iota(v("ci", 8, 32), [[2, 2], [3, 3], [0, 4]], 0, 0)
-    iota(v("ci", 32, 56), [[64, 2], [0, 3], [1024, 4]], 0, 0)
-    iota(v("ci", 56, 80), [[0, 6], [512, 4]], 0, 0)
     asel(v("blk0", 0, 128), v("ones", 0, 128), [[-16, 8], [0, 16]], ALU.is_ge, 0, 1)
     asel(v("blk", 0, 128), v("blk0", 0, 128), [[16, 8], [0, 16]], ALU.is_ge, 15, -1)
+    iota(v("ci", 0, 1), [[0, 1]], 0, 1)
     asel(IDN, v("ones", 0, 128), [[-1, 128]], ALU.is_equal, 0, 1)
-    iota(v("ai", 0, 264), [[1, 4], [4, 33], [1, 2]], 0, 0)
-    iota(v("c32", 0, 128), [[64, 2], [128, 32], [32, 2]], 0, 0)
-    iota(v("c32b", 0, 128), [[32, 128]], 0, 0)
-    iota(v("q16", 0, 8), [[2, 2], [32, 4]], 0, 0)
+    iota(v("ai", 0, 288), [[1, 9], [4, 2], [0, 16]], 0, 0)
+    iota(v("b0", 0, 64), [[128, 2], [256, 16], [16, 2]], FL + 1024 - 4096, 0)
+    iota(v("c16", 0, 256), [[16, 256]], 0, 0)
+    iota(v("q8", 0, 8), [[1, 4], [4, 2]], 0, 0)
+    ts(WB, v("blk", 0, 128), col("wtb", 0), ALU.mult)
     ts(v("ci", 1, 2), v("ci", 0, 1), 15, ALU.bitwise_and)
     copy(RHO, v("ci", 1, 2))
-    ts(R32, RHO, 32.0, ALU.mult)
-    ts(v("ci", 4, 5), v("ci", 0, 1), 1, ALU.bitwise_and)
-    ts(R1, v("ci", 4, 5), -1.0, ALU.mult)
-    ts(CA, RHO, 2.0, ALU.mult, R1, ALU.add)
-    ts(CX, CA, 32.0, ALU.mult)
-    ts(v("ci", 8, 32), v("ci", 8, 32), CA, ALU.add)
-    ts(v("ci", 8, 32), v("ci", 8, 32), 7, ALU.bitwise_and)
-    tt(v("ci", 32, 56), v("ci", 32, 56), v("ci", 8, 32), ALU.add)
-    ts(v("xoff", 0, 24), v("ci", 32, 56), CX, ALU.add)
-    tt(v("ci", 56, 80), v("ci", 56, 80), v("ci", 8, 32), ALU.add)
-    ts(v("xoff", 24, 48), v("ci", 56, 80), R32, ALU.add)
-    ts(v("ai", 0, 264), v("ai", 0, 264), 7, ALU.bitwise_and)
-    copy(v("af", 0, 264), v("ai", 0, 264))
+    ts(MCOL, v("ci", 1, 2), 2.0, ALU.mult, 1.0, ALU.add)
+    ts(R8, v("ci", 1, 2), 8.0, ALU.mult)
+    ts(Q0, v("ci", 1, 2), -float(KU), ALU.mult, float(FL), ALU.add)
+    ts(Q1, v("ci", 1, 2), -float(KU), ALU.mult, float(FL - 16 * KU + 16), ALU.add)
+    for t in range(RO):
+        ts(CMC[t], v("ci", 1, 2), -KU / 16.0, ALU.mult, float(3 * KU + 15 * KU // 16 + 1024 + AS * t), ALU.add)
+    ts(v("ai", 0, 288), v("ai", 0, 288), 7, ALU.bitwise_and)
+    ts(v("t0", 0, 288), v("ai", 0, 288), RHO, ALU.is_lt, Q0, ALU.mult)
+    for s in range(1, 4):
+        ts(v("b0", 64 * s, 64 * s + 64), v("b0", 0, 64), 32.0 * s, ALU.add)
+    for t in range(RO - 1):
+        ts(v("ba", 64 * t, 64 * t + 64), v("b0", 0, 64), 32.0 * t + 4096 + AS * t, ALU.add)
     copy(v("PF", 0, 2), v("hki", 0, 2))
     copy(v("PF", 2, 4), v("thi", 0, 2))
     copy(v("PF", 4, 6), v("wtb", 0, 2))
-    s0 = send(v("PF", 0, 6), [(t + 1, v("PR%d" % t, 0, 6), "ap%d" % t) for t in range(RO)], 3072,
-              after=[o["id"] for o in OPS if o["eng"] == "G"])
+    s0 = send(v("PF", 0, 6), [(t + 1, v("PR%d" % t, 0, 6), "ap%d" % t) for t in range(RO)], 3072)
     s = s0
     for t in range(RO - 1):
         s = send(v("Mo", 0, 2048), [(t + 1, v("M%d" % t, 0, 2048), "am%d" % t)], 1 << 19, after=[s])
         arrive("ap%d" % t, [v("PR%d" % t, 0, 6)], [(t + 1, [1, 2, 3])], [s0])
         arrive("am%d" % t, [v("M%d" % t, 0, 2048)], [(t + 1, [t + 1])], [s])
     arrive("ap2", [v("PR2", 0, 6)], [(3, [1, 2, 3])], [s0])
-    ts(WB, v("blk", 0, 128), col("PF", 4), ALU.mult)
-    ts(MCOL, RHO, 2.0, ALU.mult, 1.0, ALU.add)
-    ts(CMC, RHO, -32768.0, ALU.mult, 16 * 32768.0 + 4096.0, ALU.add)
     ts(NIDN, IDN, -1.0, ALU.mult)
     memset(v("zs", 0, 144), 0.0)
     ts(v("zs", 15, 128, 16), v("blk", 0, 128, 16), -ES, ALU.mult)
-    ts(E0, RHO, 0.0, ALU.is_equal, ES, ALU.mult)
-    ts(E1, RHO, 1.0, ALU.is_equal, ES, ALU.mult)
+    ts(E0, v("ci", 1, 2), 0.0, ALU.is_equal, ES, ALU.mult)
+    ts(E1, v("ci", 1, 2), 1.0, ALU.is_equal, ES, ALU.mult)
     ts(v("ci", 2, 3), v("thi", 0, 1), 8128, ALU.bitwise_and)
     ts(v("ci", 3, 4), v("thi", 0, 1), 63, ALU.bitwise_and)
     ts(TMPC, v("ci", 2, 3), E0, ALU.mult)
     ts(TCOL, v("ci", 3, 4), E1, ALU.mult, TMPC, ALU.add)
     ts(TB, v("blk", 0, 128), TCOL, ALU.mult)
-    for q in range(2):
-        j = v("jt", 264 * q, 264 * q + 264)
-        ts(j, v("af", 0, 264), -1.0, ALU.mult, RHO, ALU.add)
-        th = v("PV%d" % q, 0, 264)
-        if q == 0:
-            ts(th, j, 0.0, ALU.is_le, 3.0e7, ALU.mult)
-            ts(j, j, -3.0, ALU.add, 0.0, ALU.max)
-            ts(j, j, float(2 ** 19), ALU.mult, 32768.0, ALU.add)
-            tt(th, j, th, ALU.add)
-        else:
-            ts(th, j, float(2 ** 19), ALU.mult, 13.0 * 2 ** 19 + 32768.0, ALU.add)
     memset(v("m16", 0, 64), 1.0)
     memset(v("m16", 0, 64, 16), 0.0)
-    memset(v("m32", 0, 1024), 1.0)
-    memset(v("m32", 0, 1024, 32), 0.0)
+    memset(v("m32", 0, 512), 1.0)
+    memset(v("m32", 0, 512, 32), 0.0)
     ts(BK, v("blk", 0, 128), BIG, ALU.mult)
     ts(BKN, v("blk", 0, 128), -BIG, ALU.mult)
-    ts(v("c32p", 0, 128), v("c32", 0, 128), 4096.0, ALU.add)
+    memset(v("cst", 384, 512), float(FL))
     for t in range(RO):
-        memset(v("cst", 64 * t, 64 * t + 64), -4096.0 * (t + 1))
-        ts(v("wj", 128 * t, 128 * t + 128), v("blk", 0, 128), col("PR%d" % t, 5), ALU.mult)
+        pr = "PR%d" % t
+        memset(v("cst", 128 * t, 128 * t + 128), 1024.0 - 4096.0 * (t + 2))
+        ts(v("wj", 128 * t, 128 * t + 128), v("blk", 0, 128), col(pr, 5), ALU.mult)
+        ts(KT[t], col(pr, 1), 895.5, ALU.is_ge, -65536.0, ALU.mult)
+        ts(KAP[t], col(pr, 1), 32.0, ALU.mult, KT[t], ALU.add)
     for t in range(RO - 1):
-        ts(v("zw", 144 * t, 144 * t + 144), v("zs", 0, 144), col("PR%d" % t, 5), ALU.mult, -1.0 / ES, ALU.mult)
+        ts(v("zw", 144 * t, 144 * t + 144), v("zs", 0, 144), col("PR%d" % t, 5), ALU.mult, -128.0 / ES, ALU.mult)
 
 
 def slot(name, h, k, w=1):
-    return v("%s%d" % (name, h), n * k, n * (k + w))
+    return v("%s%d" % (name, h), NG[h] * k, NG[h] * (k + w))
 
 
-def pv(h, k):
-    return v("PV%d" % h, 320 + n * k, 320 + n * (k + 1))
+def own(h, k, w=1):
+    if OWN:
+        lo = 4 * sum(NG[:h]) + NG[h] * k
+        return v("PV", lo, lo + NG[h] * w)
+    return slot("F", h, 14 + k, w)
 
 
-def hash16(h, si, kcol, bound, out16):
-    u, uu, p = slot("I", h, 1), slot("I", h, 2), slot("I", h, 3)
-    ts(u, si, 4095, ALU.bitwise_and)
-    tt(uu, u, u, ALU.mult)
-    ts(pv(h, 0), u, kcol, ALU.mult)
-    ts(uu, uu, 5, ALU.arith_shift_right)
-    tt(uu, uu, pv(h, 0), ALU.add)
-    ts(p, uu, bound - 1, ALU.bitwise_and)
-    copy(out16, p)
+def pieces(total):
+    k = min(CFG["piece"], total)
+    return [(lo, lo + k) for lo in range(0, total, k)]
+
+
+def gather(out, win, lst):
+    for lo, hi in pieces(count(out)):
+        move(sub(out, lo, hi), ind(win, sub(lst, lo // 16, hi // 16)))
 
 
 def diffs(h, y, src, dst):
-    for b, bank in enumerate(("PA", "PB")):
-        reg = [v("%s%d" % (bank, h), n * k, n * (k + 1)) for k in range(8)]
-        gs = [v(src, 8 * b + k, 16 * n, 16) for k in range(8)]
+    n = NG[h]
+    if n == 32:
+        bank = "PA%d" % h
+        mm([(v(bank, m, 512, 16), NIDN, y) for m in range(16)], True, False)
+        ps = pieces(512)
+        for lo, hi in ps:
+            mm([(v(bank, lo, hi), IDN, sub(src, lo, hi))], False, hi == 512)
+        act(dst, v(bank, 0, 512), ACT.Abs)
+        return [sub(dst, m, 512, 16) for m in range(16)]
+    for b, bank in enumerate(("PA%d" % h, "PB%d" % h)):
+        reg = [v(bank, n * k, n * (k + 1)) for k in range(8)]
         mm([(reg[k], NIDN, y) for k in range(8)], True, False)
-        mm([(reg[k], IDN, gs[k]) for k in range(8)], False, True)
-        act(v(dst, 512 * b, 512 * b + 512), v("%s%d" % (bank, h), 0, 512), ACT.Abs)
+        mm([(reg[k], IDN, sub(src, 8 * b + k, 16 * n, 16)) for k in range(8)], False, True)
+        act(sub(dst, 512 * b, 512 * b + 512), v(bank, 0, 512), ACT.Abs)
+    return [sub(dst, n * m, n * m + n) for m in range(16)]
 
 
 def zsel(name, base, m):
     return v(name, base + 15 - m, base + 143 - m)
 
 
+def sums(out, first, by_m):
+    k = 16 if count(out) == 32 or by_m[0][3] != 1 else 8
+    mm(first + [(out, zsel("zs", 0, m), by_m[m]) for m in range(k)], True, k == 16)
+    if k < 16:
+        mm([(out, zsel("zs", 0, m), by_m[m]) for m in range(k, 16)], False, True)
+
+
 def flanks(t, h):
-    w0 = XOFF - 4096 * t
-    awin = v("W", AOFF, WEND)
-    xa = slot("X", h, 0) if t == 0 else slot("X", h, 2 + t)
-    beta = v("c32", n * h, n * h + n) if t == 0 else slot("F", h, 0)
-    ps = "PS%d" % h
-    si, u, p, lq = slot("I", h, 0), slot("I", h, 1), slot("I", h, 3), slot("I", h, 4)
-    ba = pv(h, 1)
-    sh = phase(t, h)
+    n = NG[h]
+    nb = n // 16
+    ps, pa = "PS%d" % h, "PA%d" % h
+    w0 = tbase(t - 1, h)
+    awin = v("W", abase(t), abase(t) + AS)
+    si, u, uu, p, lq = [slot("I", h, k) for k in range(5)]
     if t == 0:
-        move(slot("X", h, 0, 3), ind(v("W", XOFF, AOFF), v("xoff", 12 * h, 12 * h + 12)))
-        mm([(v(ps, 0, n), WB, xa)])
+        def x0(r, b):
+            lo = XOFF + 32 * gene0(h, b) + place(r, h, b)
+            return v("W", lo, lo + 15 * 256 + 1, 256)
+        mm([(v(ps, 16 * b, 16 * b + 16), WB, x0(0, b)) for b in range(nb)])
         copy(si, v(ps, 0, n))
+        mm([(v(pa, n * r + 16 * b, n * r + 16 * b + 16), IDN, x0(r, b)) for r in range(RO) for b in range(nb)])
+        act(slot("X", h, 0, 3), v(pa, 0, 3 * n), ACT.Identity)
+        beta = v("b0", 64 * CH[h][0], 64 * CH[h][0] + 2 * n)
     else:
-        tt(si, v(ps, 0, n), slot("F", h, 1), ALU.min)
-    tt(ba, beta, v("af", sh, sh + n), ALU.add)
-    hash16(h, si, col("PF", 0), 4096, slot("U", h, 0))
-    xo, key = slot("F", h, 2), slot("F", h, 5)
+        beta = own(h, 2, 2)
+    xa = slot("X", h, (0, 3, 5)[t])
+    at = 32 * place(t, h, 0)
+    la, xo, f3, key = slot("F", h, 3), slot("F", h, 4), slot("F", h, 5), slot("F", h, 6)
+    ts(u, si, 4095, ALU.bitwise_and)
+    tt(uu, u, u, ALU.mult)
     ts(lq, u, MCOL, ALU.mult)
+    ts(own(h, 0), u, col("PF", 0), ALU.mult)
+    ts(uu, uu, 5, ALU.arith_shift_right)
     ts(lq, lq, 4, ALU.arith_shift_right, 15, ALU.bitwise_and)
-    tt(xo, lq, ba, ALU.add)
-    ts(slot("U", h, 2), xo, 4.0 + 4096 * t, ALU.add)
-    tt(pv(h, 2), p, ba, ALU.subtract)
-    tt(slot("F", h, 3), xo, pv(h, 2), ALU.add)
-    ts(slot("U", h, 1), slot("F", h, 3), 4.0, ALU.add)
-    ts(slot("F", h, 4), lq, float(2 ** 19), ALU.mult, CMC, ALU.add)
-    tt(key, slot("F", h, 4), pv(h, 2), ALU.add)
+    tt(uu, uu, own(h, 0), ALU.add)
+    tt(la, lq, v("ai", at, at + n), ALU.add)
+    ts(p, uu, 4095, ALU.bitwise_and)
+    tt(xo, la, sub(beta, 0, 2 * n, 2), ALU.add)
+    copy(slot("U", h, 0), p)
+    ts(slot("U", h, 2), xo, float(AOFF - FL - 1024 - w0 + 4), ALU.add)
+    tt(f3, p, lq, ALU.add)
+    ts(slot("U", h, 1), f3, 4.0, ALU.add)
+    ts(own(h, 1), la, float(KU - 1), ALU.mult, CMC[t], ALU.add)
+    tt(key, f3, own(h, 1), ALU.add)
     if t < RO - 1:
-        xn = slot("X", h, 1) if t == 0 else slot("X", h, 5)
-        mm([(v(ps, n, 2 * n), WB, xn)])
-        act(slot("F", h, 1), v(ps, n, 2 * n), ACT.Identity, bias=float(2 ** 21))
-    G, E, D, AA, AB, U = ["%s%d" % (x, h) for x in ("G", "E", "D", "AA", "AB", "U")]
-    for k in range(2):
-        move(v(G, 512 * k, 512 * k + 512), ind(awin, v(U, 32 * k, 32 * k + 32)))
-    for k in range(2):
-        move(v(E, 512 * k, 512 * k + 512), ind(v("W", w0, AOFF), v(U, 2 * n + 32 * k, 2 * n + 32 * k + 32)))
-    diffs(h, xa, G, AA)
-    e1, e2 = v(ps, 2 * n, 3 * n), v(ps, 3 * n, 4 * n)
-    mm([(e1, TB, v("ones", 0, n))] + [(e1, zsel("zs", 0, m), v(AA, n * m, n * m + n)) for m in range(8)], True, False)
-    mm([(e1, zsel("zs", 0, m), v(AA, n * m, n * m + n)) for m in range(8, 16)], False, True)
-    tt(slot("F", h, 4), key, e1, ALU.min)
-    for k in range(2):
-        tt(v(D, 512 * k, 512 * k + 512), ind(awin, v(U, n + 32 * k, n + 32 * k + 32)), v(E, 512 * k, 512 * k + 512),
-           ALU.subtract)
-        act(v(AB, 512 * k, 512 * k + 512), v(D, 512 * k, 512 * k + 512), ACT.Abs)
-    mm([(e2, TB, v("ones", 0, n))] + [(e2, zsel("zs", 0, m), v(AB, m, 16 * n, 16)) for m in range(16)])
-    k2, tr, s1 = slot("F", h, 5), slot("F", h, 6), slot("F", h, 7)
-    tt(k2, slot("F", h, 4), e2, ALU.min)
-    vtr(tr, k2)
+        mm([(v(ps, n, 2 * n), WB, slot("X", h, (1, 4)[t]))])
+        act(slot("F", h, 2), v(ps, n, 2 * n), ACT.Identity, bias=float(2 ** 21))
+    G, E, D = [slot(x, h, 0, 16) for x in "GED"]
+    AA, AB = slot("A", h, 0, 16), slot("A", h, 16, 16)
+    gather(E, v("W", w0, AOFF), slot("U", h, 2))
+    gather(G, awin, slot("U", h, 0))
+    d1 = diffs(h, xa, G, AA)
+    both = CFG["both"] and n == 32
+    e1, e2 = v(ps, 2 * n, 3 * n), v(ps, 3 * n, 4 * n) if both else v(pa, 0, n)
+    if not both:
+        sums(e1, [(e1, TB, v("ones", 0, n))], d1)
+        tt(key, key, e1, ALU.min)
+    for lo, hi in pieces(16 * n):
+        tt(sub(D, lo, hi), ind(awin, sub(slot("U", h, 1), lo // 16, hi // 16)), sub(E, lo, hi), ALU.subtract)
+        act(sub(AB, lo, hi), sub(D, lo, hi), ACT.Abs)
+    if both:
+        e12 = v(ps, 2 * n, 4 * n)
+        sums(e12, [(e12, TB, v("ones", 0, 2 * n))], [sub(slot("A", h, 0, 32), m, 32 * n, 16) for m in range(16)])
+        tt(key, key, e1, ALU.min)
+    else:
+        sums(e2, [(e2, TB, v("ones", 0, n))], [sub(AB, m, 16 * n, 16) for m in range(16)])
+    tr, s1, s2, best = slot("F", h, 7), slot("F", h, 8), slot("F", h, 9), own(h, 1)
+    tt(key, key, e2, ALU.min)
+    vtr(tr, key)
     scan(s1, v("m16", 0, n), tr)
-    s2, best, dl = slot("I", h, 5), slot("I", h, 6), slot("I", h, 7)
     scan((s2[0], s2[1], s2[2], -1), v("m16", 0, n), (s1[0], s1[1], s1[2], -1))
     vtr(best, s2)
-    ts(dl, best, 32767, ALU.bitwise_and)
-    for q in range(2):
-        mk = pv(h, 2 * q)
-        tt(mk, best, v("PV%d" % q, sh, sh + n), ALU.is_ge)
-        tt(mk, dl, mk, ALU.mult)
-        tt(slot("F", h, 8 + q), beta, mk, ALU.add)
-        ts(v(U, 4 * n + q, 6 * n, 2), slot("F", h, 8 + q), RHO, ALU.add, 16.0 * q + 4096 * t, ALU.add)
-    t0 = w0 - 4096 + 2048 * h
-    lo = 0
-    for k in CFG["tg"]:
-        move(v("W", t0 + lo, t0 + lo + k), ind(v("W", w0, WEND), v(U, 4 * n + lo // 16, 4 * n + (lo + k) // 16)))
-        scan(v("SO%d" % h, lo, lo + k), v("m32", 0, k), v("W", t0 + lo, t0 + lo + k))
-        lo += k
+    z, f = slot("I", h, 5, 2), slot("F", h, 10, 2)
+    tt(sub(z, 0, 2 * n, 2), best, v("t0", at, at + n), ALU.add)
+    ts(sub(z, 1, 2 * n, 2), best, Q1, ALU.add)
+    ts(z, z, FL + KU // 16 - 1, ALU.bitwise_and)
+    tt(f, z, beta, ALU.max)
+    ts(slot("U", h, 4, 2), f, RHO, ALU.add, float(AOFF - FL - 1024 - w0), ALU.add)
+    t0 = tbase(t, h)
+    for lo, hi in pieces(32 * n):
+        move(v("W", t0 + lo, t0 + hi), ind(v("W", w0, abase(t) + AS), sub(slot("U", h, 4, 2), lo // 16, hi // 16)))
+        scan(v("SO%d" % h, lo, hi), v("m32", 0, hi - lo), v("W", t0 + lo, t0 + hi))
 
 
 def verdict(t, h):
-    w0 = XOFF - 4096 * t
-    t0 = w0 - 4096 + 2048 * h
-    ps, pa, pb = "PS%d" % h, "PA%d" % h, "PB%d" % h
+    n = NG[h]
+    nb = n // 16
+    s0 = CH[h][0]
+    t0 = tbase(t, h)
+    ps, pa = "PS%d" % h, "PA%d" % h
     z = v("SO%d" % h, 31, 32 * n, 32)
-    G, AA, U = "G%d" % h, "AA%d" % h, "U%d" % h
-    pr = "PR%d" % t
-    si = slot("I", h, 0)
-    mm([(v(ps, 4 * n, 5 * n), v("wj", 128 * t, 128 * t + 128), z)])
-    copy(si, v(ps, 4 * n, 5 * n))
-    hash16(h, si, col(pr, 1), 2048, slot("U", h, 3))
+    G, AA = slot("G", h, 0, 16), slot("A", h, 0, 16)
+    si, u, uu, p = [slot("I", h, k) for k in range(4)]
+    mm([(v(ps, 0, n), v("wj", 128 * t, 128 * t + 128), z)])
+    copy(si, v(ps, 0, n))
+    ts(u, si, 4095, ALU.bitwise_and)
+    ts(own(h, 0), u, KAP[t], ALU.add)
+    tt(uu, u, own(h, 0), ALU.mult)
+    ts(p, uu, 5, ALU.arith_shift_right, 2047, ALU.bitwise_and)
+    copy(slot("U", h, 3), p)
     if t < RO - 1:
-        move(slot("X", h, 6, 2 - t), ind(v("W", t0, t0 + 2048), v("xoff", 24 + 12 * h + 4 * t + 4, 36 + 12 * h)))
-        asel(v("zc%d" % t, n * h, n * h + n), z, [[0, n]], ALU.is_ge, 0, 0)
-        if h == NCH - 1:
-            memory_write(t)
-    for k in range(2):
-        move(v(G, 512 * k, 512 * k + 512), ind(v("M%d" % t, 0, 2048), v(U, 3 * n + 32 * k, 3 * n + 32 * k + 32)))
-    diffs(h, z, G, AA)
-    dm = v(ps, 5 * n, 6 * n)
-    mm([(dm, zsel("zs", 0, m), v(AA, n * m, n * m + n)) for m in range(8)], True, False)
-    mm([(dm, zsel("zs", 0, m), v(AA, n * m, n * m + n)) for m in range(8, 16)], False, True)
-    hit = slot("X", h, 8)
-    act(hit, dm, ACT.Relu, bias=col(pr, 3), scale=1.0 / ES)
-    cb = v(pa, 0, n)
+        asel(v("zc%d" % t, 32 * s0, 32 * s0 + n), z, [[0, n]], ALU.is_ge, 0, 0)
+        if h == CFG["order"][t][-1]:
+            memory_write(t, h)
+    gather(G, v("M%d" % t, 0, 2048), slot("U", h, 3))
+    dm = v(ps, 3 * n, 4 * n)
+    sums(dm, [], diffs(h, z, G, AA))
+    hit = slot("X", h, 6)
+    act(hit, dm, ACT.Relu, bias=col("PR%d" % t, 3), scale=1.0 / ES)
+
+    def new(r, b):
+        lo = t0 + 512 * b + place(r, h, b)
+        return v("W", lo, lo + 15 * 32 + 1, 32)
+    cb, sn = v(pa, 0, 2 * n), v(pa, 2 * n, 3 * n)
+    c0 = (t0 % 4096) // 16
+    pre = [(cb, IDN, v("c16", c0, c0 + 2 * n)), (cb, IDN, v("cst", 128 * t, 128 * t + 2 * n)),
+           (cb, IDN, v("cst", 384, 384 + 2 * n))]
+    post = [(sub(cb, q, 2 * n, 2), BK, hit) for q in range(2)]
     if t < RO - 1:
-        mm([(v(ps, 0, n), WB, slot("X", h, 6)), (v(ps, 0, n), BK, hit)])
-    mm([(cb, IDN, v("c32b", n * h, n * h + n)), (cb, IDN, v("cst", 64 * t, 64 * t + n)), (cb, BK, hit)])
-    beta = v("c32", n * h, n * h + n) if t == 0 else slot("F", h, 0)
-    if t < RO - 1 and h == 0:
-        ta = v("F0", 10 * n, 10 * n + 32)
-        tt(ta, v(pa, t, n, 2), v("c32p", t, n, 2), ALU.min)
-        for q in range(2):
-            ts(v(U, 6 * n + q, 7 * n, 2), ta, RHO, ALU.add, 16.0 * q + 4096 * (t + 1), ALU.add)
-        for k in range(2):
-            move(v("tmp", 512 * k, 512 * k + 512), ind(v("W", w0 - 4096, WEND), v(U, 6 * n + 32 * k, 6 * n + 32 * k + 32)))
-    tt(slot("F", h, 0), beta, cb, ALU.min)
+        pre += [(sub(sn, 16 * b, 16 * b + 16), WB, new(t + 1, b)) for b in range(nb)]
+        post += [(sn, BK, hit)]
+    mm(pre, True, False)
+    mm(post, False, True)
+    beta = v("b0", 64 * s0, 64 * s0 + 2 * n) if t == 0 else slot("F", h, 0, 2)
     if t < RO - 1:
-        for b, lo in ((BK, 0), (BKN, 2 * n)):
-            for j in range(2 - t):
-                reg = v(pb, lo + n * j, lo + n * j + n)
-                mm([(reg, IDN, slot("X", h, 6 + j)), (reg, b, hit)])
-        pairs = [(3, 1), (5, 2)] if t == 0 else [(4, 5)]
-        for j, (new, old) in enumerate(pairs):
-            tt(slot("X", h, new), slot("X", h, old), v(pb, n * j, n * j + n), ALU.min)
-            tt(slot("X", h, new), slot("X", h, new), v(pb, 2 * n + n * j, 3 * n + n * j), ALU.max)
+        if s0 <= t < s0 + CH[h][1]:
+            ta, lst = v("F%d" % h, 12 * n, 12 * n + 64), v("U%d" % h, 6 * n, 6 * n + 64)
+            tt(ta, sub(cb, 64 * (t - s0), 64 * (t - s0) + 64), v("ba", 64 * t, 64 * t + 64), ALU.min)
+            ts(lst, ta, RHO, ALU.add, float(AOFF - FL - 1024 - t0), ALU.add)
+        tt(slot("I", h, 0), sn, slot("F", h, 2), ALU.min)
+        if OWN:
+            tt(own(h, 2, 2), beta, cb, ALU.min)
+            if t == 0:
+                tt(slot("F", h, 0, 2), beta, cb, ALU.min)
+        else:
+            tt(own(h, 2, 2), beta if t == 0 else own(h, 2, 2), cb, ALU.min)
+        if s0 <= t < s0 + CH[h][1]:
+            archive_write(t, v("W", t0, abase(t) + AS), lst)
+        k = RO - 1 - t
+        lo, hi = v(ps, 4 * n, (4 + k) * n), v(ps, 6 * n, (6 + k) * n)
+        mm([(sub(reg, n * j + 16 * b, n * j + 16 * b + 16), IDN, new(t + 1 + j, b))
+            for reg in (lo, hi) for j in range(k) for b in range(nb)] +
+           [(sub(reg, n * j, n * j + n), mat, hit) for reg, mat in ((lo, BK), (hi, BKN)) for j in range(k)])
+        old, sel = (slot("X", h, 1, 2), slot("X", h, 3, 2)) if t == 0 else (slot("X", h, 4), slot("X", h, 5))
+        tt(sel, old, lo, ALU.min)
+        tt(sel, sel, hi, ALU.max)
     else:
-        for j in range(2):
-            for q in range(2):
-                ts(v("yo", 4 * h + 2 * j + q, 256, 8), v("F%d" % h, j, n, 2), RHO, ALU.add,
-                   16.0 * q + 4096 * RO, ALU.add)
-        if h == NCH - 1:
-            for lo in range(0, 4096, 512):
-                move(v("Y", lo, lo + 512), ind(v("W", 0, AOFF), v("yo", lo // 16, lo // 16 + 32)))
-                if lo % 1024:
-                    dma("Y", v("y", lo - 512, lo + 512), v("Y", lo - 512, lo + 512), 256 * 1024)
+        f, lst = slot("F", h, 10, 2), slot("U", h, 8, 2)
+        if OWN:
+            copy(slot("F", h, 0, 2), own(h, 2, 2))
+        tt(f, slot("F", h, 0, 2) if OWN else own(h, 2, 2), cb, ALU.min)
+        ts(lst, f, RHO, ALU.add, float(AOFF - FL - 1024 - t0), ALU.add)
+        k = 16 // CFG["ypiece"]
+        for r0 in range(0, 16, k):
+            for b in range(nb):
+                c = 32 * gene0(h, b)
+                part = v("SO%d" % h, 512 * b + 32 * r0, 512 * b + 32 * (r0 + k))
+                move(part, ind(v("W", t0, AOFF), sub(lst, 32 * b + 2 * r0, 32 * b + 2 * r0 + 2 * k)))
+                move(rows("Y", r0, r0 + k, c, c + 32), part)
+            if h == CFG["order"][t][-1]:
+                dma("Y", v("y", 256 * r0, 256 * (r0 + k)), rows("Y", r0, r0 + k, 0, 256))
 
 
-def memory_write(t):
+def memory_write(t, h):
     zc, so = "zc%d" % t, "so%d" % t
-    sc = v("PS1", 6 * n, 6 * n + 8)
+    sc = v("PS%d" % h, NG[h], NG[h] + 8)
     mm([(sc, zsel("zw", 144 * t, r), v(zc, r, 128, 16)) for r in range(16)])
     copy(v("si", 0, 8), sc)
-    ts(v("si", 8, 16), v("si", 0, 8), 15, ALU.bitwise_and)
-    ts(v("sf", 0, 8), v("si", 8, 16), 128.0, ALU.mult, CA, ALU.add)
-    tt(v("sf", 8, 16), v("sf", 0, 8), v("q16", 0, 8), ALU.add)
-    copy(v(so, 0, 8), v("sf", 8, 16))
+    ts(v("si", 8, 16), v("si", 0, 8), 2047, ALU.bitwise_and)
+    tt(v("sf", 0, 8), v("si", 8, 16), v("q8", 0, 8), ALU.add)
+    ts(v(so, 0, 8), v("sf", 0, 8), R8, ALU.add)
     lands = [(1, 0), (2, 1)] if t == 0 else [(1, 2)]
     backs = [b for b, k in lands]
     a = send(v(zc, 0, 128), [(b, v("zl%d" % k, 0, 128), "az%d" % k) for b, k in lands], 32768)
@@ -529,26 +609,31 @@ def memory_write(t):
         copy(ind(v("M%d" % (1 if k == 0 else 2), 0, 2048), v("sl%d" % k, 0, 8)), v("zl%d" % k, 0, 128))
 
 
-def archive_write(t):
-    for k in range(32):
-        a0 = AOFF + 128 * k + 32 * t
-        move(v("W", a0, a0 + 32), v("tmp", 32 * k, 32 * k + 32))
+def archive_write(t, win, lst):
+    nxt = abase(t + 1)
+    dst = [(i, nxt + 32 * (8 * (i % 16) + 4 * (i // 16) + t)) for i in range(32)]
     if t == 0:
-        move(v("W", PAD, PAD + 32), v("tmp", 0, 32))
+        dst.append((0, nxt + 4096))
+    if CFG["arch"] == "tmp":
+        gather(v("tmp", 0, 1024), win, lst)
+    for i, a0 in dst:
+        if CFG["arch"] == "tmp":
+            move(v("W", a0, a0 + 32), v("tmp", 32 * i, 32 * i + 32), CFG["gcopy"])
+        else:
+            move(v("W", a0, a0 + 32), ind(win, sub(lst, 2 * i, 2 * i + 2)))
+    if t == 0:
+        dma("Y", v("W", abase(2), abase(2) + AS), v("W", nxt, nxt + AS))
 
 
 def build():
     setup()
     for t in range(RO):
-        for h in range(NCH):
+        for h in CFG["order"][t]:
             TAG[0] = (t, h)
             flanks(t, h)
-        for h in range(NCH):
+        for h in CFG["order"][t]:
             TAG[0] = (t, h)
             verdict(t, h)
-        if t < RO - 1:
-            TAG[0] = (t, 0)
-            archive_write(t)
     seen = {}
     for o in OPS:
         dep = dict((d, False) for d in o["after"])
@@ -569,16 +654,28 @@ def build():
             OPS[d]["succ"].append(o["id"])
 
 
-def priorities(bias):
+def price(M):
+    out = []
+    for o in OPS:
+        if o["kind"] == "c":
+            out.append(dict((e, c[0] + M["cy"] * (c[1] + M["g"] * c[2] + M["sc"] * c[3]) + M["pcy"] * c[4])
+                            for e, (f, c) in o["alt"].items()))
+        else:
+            out.append(dict((e, c) for e, (f, c) in o["alt"].items()))
+    return out
+
+
+def priorities(M, cost):
     prio = [0.0] * len(OPS)
     for o in OPS[::-1]:
-        span = o["cost"]
+        span = min(cost[o["id"]].values())
         if o["kind"] == "d":
-            span = LAT["dma"] + o["cost"] / LAT["rate"]
+            span = M["dma"] + span / M["rate"]
         if o["kind"] == "r":
-            span = 1000.0 + LAT["rem"] + o["cost"] / LAT["rrate"]
-        prio[o["id"]] = span + LAT["cross"] + max([prio[s] for s in o["succ"]] + [0.0])
-    return [prio[o["id"]] + (bias if o["tag"] is None or o["tag"][1] == 0 else 0.0) for o in OPS]
+            span = M["riss"] + M["rem"] + span / M["rrate"]
+        prio[o["id"]] = span + M["cross"] + max([prio[s] for s in o["succ"]] + [0.0])
+    return [prio[o["id"]] - (CFG["bias"] * CFG["order"][o["tag"][0]].index(o["tag"][1]) if o["tag"] else 0.0)
+            for o in OPS]
 
 
 def nudge(prio, seed):
@@ -591,14 +688,28 @@ def nudge(prio, seed):
     return prio[:a] + [x + d for x in prio[a:a + k]] + prio[a + k:]
 
 
-def schedule(prio, delta, pen):
+def occupy(M, o, e, t, c, st):
+    if o["kind"] == "d":
+        st[0] = max(st[0], t + M["issue"]) + c / M["rate"]
+        return t + M["issue"], st[0] + M["dma"]
+    if o["kind"] == "r":
+        free = t + M["riss"] + (0.0 if st[1] else M["rfirst"])
+        st[1] = max(st[1], free) + c / M["rrate"]
+        return free, st[1] + M["rem"]
+    if o["kind"] == "x":
+        return t, t
+    return t + c, t + c
+
+
+def schedule(prio, M, cost):
     N = len(OPS)
+    delta, pen = CFG["delta"], CFG["pen"]
     left = [len(o["dep"]) for o in OPS]
     ready = [dict((e, 0.0) for e in o["alt"]) for o in OPS]
     fin = [0.0] * N
     beg = [0.0] * N
     free = dict((e, 0.0) for e in "VSPGYX")
-    dma_free = [0.0, 0.0]
+    st = [0.0, 0.0]
     cand = [i for i in range(N) if left[i] == 0]
     order = dict((e, []) for e in "VSPGYX")
     while cand:
@@ -608,25 +719,17 @@ def schedule(prio, delta, pen):
         if e == "Y":
             pick = min(able)
         else:
-            pick = max(able, key=lambda i: (prio[i] - (pen if e == "V" and OPS[i]["eng"] == "F" else 0.0), -i))
+            def rank(i):
+                return prio[i] - (pen if e == "V" and OPS[i]["eng"] == "F" else 0.0), -i
+            pick = max(able, key=rank)
+            end = ready[pick][e] + CFG["slack"]
+            fill = [i for i in able if max(ready[i][e], t0) + cost[i][e] <= end]
+            if fill and ready[pick][e] > t0:
+                pick = max(fill, key=rank)
         o = OPS[pick]
         t = max(ready[pick][e], free[e])
-        cost = o["alt"][e][1]
         beg[pick] = t
-        if o["kind"] == "d":
-            free[e] = t + LAT["issue"]
-            if e == "Y":
-                dma_free[0] = max(dma_free[0], free[e]) + cost / LAT["rate"]
-            fin[pick] = (dma_free[0] if e == "Y" else t) + LAT["dma"]
-        elif o["kind"] == "r":
-            free[e] = t + 1000.0
-            dma_free[1] = max(dma_free[1], free[e]) + cost / LAT["rrate"]
-            fin[pick] = dma_free[1] + LAT["rem"]
-        elif o["kind"] == "x":
-            fin[pick] = t
-        else:
-            free[e] = t + cost
-            fin[pick] = free[e]
+        free[e], fin[pick] = occupy(M, o, e, t, cost[pick][e], st)
         order[e].append(pick)
         cand.remove(pick)
         for j in o["succ"]:
@@ -637,7 +740,7 @@ def schedule(prio, delta, pen):
                 elif not OPS[j]["dep"][pick]:
                     at = fin[pick]
                 else:
-                    at = fin[pick] + (LAT["same"] if q == e else LAT["cross"])
+                    at = fin[pick] + (M["same"] if q == e else M["cross"])
                 if at > r[q]:
                     r[q] = at
             left[j] -= 1
@@ -647,10 +750,11 @@ def schedule(prio, delta, pen):
 
 
 def plan():
-    prio = priorities(CFG["bias"])
+    cost = price(MODEL)
+    prio = priorities(MODEL, cost)
     for s in CFG["steps"]:
         prio = nudge(prio, s)
-    return schedule(prio, CFG["delta"], CFG["pen"])
+    return schedule(prio, MODEL, cost)
 
 
 build()

@@ -1,3 +1,5 @@
+import math
+
 from concourse.bass import DstId, RemoteDMATransfer
 from concourse.mybir import AluOpType, ActivationFunctionType
 
@@ -10,14 +12,14 @@ XOFF, AOFF, AS = 12288, 16384, 4128
 WEND = AOFF + RO * AS
 BIG = float(2 ** 22)
 ES = float(2 ** 25)
-KU = 2 ** 18
-FL = 2 ** 23
+MU = 2 ** 15
+KU = 17 * MU
 
-CFG = {"chunks": [(0, 2), (2, 2)], "order": [[0, 1], [0, 1], [0, 1]], "piece": 512, "both": False,
-       "arch": "tmp", "gcopy": True, "ypiece": 2, "bias": 2000.0, "delta": 250.0, "pen": 6000.0, "slack": 100.0,
-       "steps": [12, 16, 30, 37, 55, 65, 68, 69, 123, 137, 138, 139, 145, 146, 155, 183, 197, 217, 220, 281, 309, 313, 326, 336, 349, 350, 391, 398, 403, 423, 459, 537, 671, 714, 786, 796, 867, 871, 927, 946, 997, 999, 1006, 1032, 1045, 1057, 1130, 1183, 1367, 1370, 1380, 1442, 1660, 1734, 1837, 1850, 1987, 2375]}
-MODEL = {"cy": 0.9, "g": 1.56, "sc": 3.8, "pcy": 0.5, "same": 220.0, "cross": 240.0, "issue": 60.0, "dma": 1300.0,
-         "rate": 330.0, "riss": 700.0, "rfirst": 2500.0, "rem": 1800.0, "rrate": 70.0}
+CFG = {"chunks": [(0, 1), (1, 1), (2, 2)], "order": [[0, 1, 2], [1, 0, 2], [2, 1, 0]], "piece": 512, "both": False,
+       "arch": "tmp", "ba": True, "gy": True, "gcopy": True, "ypiece": 4, "late": True, "loads": "gma",
+       "bias": 2000.0, "delta": 60.0, "pen": 6000.0, "slack": 100.0, "moves": 250000, "seed": 1, "heat": (40.0, 2.0)}
+MODEL = {"cy": 0.85, "g": 1.56, "sc": 3.8, "pcy": 0.45, "same": 220.0, "cross": 260.0, "issue": 60.0, "dma": 1100.0,
+         "rate": 420.0, "riss": 700.0, "rfirst": 2500.0, "rem": 1800.0, "rrate": 70.0}
 
 CH = CFG["chunks"]
 NG = [32 * w for s, w in CH]
@@ -28,11 +30,11 @@ SEMAPHORES = ["cV", "cS", "cP", "cG", "sent"]
 for _dt, _list in [
     ("bfloat16", [("W", WEND), ("Mo", 2048), ("M0", 2048), ("M1", 2048), ("M2", 2048), ("wtb", 8),
                   ("ones", 128), ("blk0", 128), ("blk", 128), ("idn", 128), ("nidn", 128), ("bk", 128), ("bkn", 128),
-                  ("wb", 128), ("tb", 128), ("wj", 384), ("zs", 144), ("zw", 288), ("c16", 256), ("cst", 512),
+                  ("wb", 128), ("tb", 128), ("wj", 384), ("zs", 144), ("zw", 288), ("wl", 128), ("c32", 128), ("cst", 128),
                   ("m32", 1024), ("tmp", 1024), ("zc0", 128), ("zc1", 128), ("zl0", 128), ("zl1", 128), ("zl2", 128)]),
-    ("float32", [("PF", 8), ("PR0", 8), ("PR1", 8), ("PR2", 8), ("b0", 256), ("ba", 128), ("t0", 288), ("cf", 32),
+    ("float32", [("PF", 8), ("PR0", 8), ("PR1", 8), ("PR2", 8), ("b0", 128), ("ba", 64), ("t0", 288), ("cf", 32),
                  ("m16", 64), ("q8", 8), ("sf", 8)]),
-    ("int32", [("hki", 4), ("thi", 4), ("ai", 288), ("ci", 8), ("si", 16)]),
+    ("int32", [("hki", 4), ("thi", 4), ("ai", 288), ("wi", 128), ("ci", 8), ("si", 16)]),
     ("uint16", [("so0", 8), ("so1", 8), ("sl0", 8), ("sl1", 8), ("sl2", 8)]),
 ]:
     for _nm, _cols in _list:
@@ -217,7 +219,7 @@ def asel(out, in_, pattern, op, base, cm):
     return add({"G": g_sel(out, in_, pattern, op, base, cm)}, [in_], [out])
 
 
-def dma(eng, out, in_, after=()):
+def dma(eng, out, in_, after=(), behind=False):
     sem = "d%d" % len(SEMAPHORES)
     SEMAPHORES.append(sem)
     side = in_ if out[0] in INPUTS else out
@@ -226,8 +228,10 @@ def dma(eng, out, in_, after=()):
     def fn(c):
         q = c["g"].sync if eng == "Y" else c["g"].scalar
         return q.dma_start(arg(c["T"], out), arg(c["T"], in_))
-    return add({eng: (fn, nbytes)}, [] if in_[0] in INPUTS else [in_], [] if out[0] in INPUTS else [out], "d", sem,
-               after=after)
+    i = add({eng: (fn, nbytes)}, [] if in_[0] in INPUTS else [in_], [] if out[0] in INPUTS else [out], "d", sem,
+            after=after if behind else ())
+    OPS[i]["wait"] = [] if behind else list(after)
+    return i
 
 
 def share(c, backs):
@@ -291,7 +295,7 @@ RHO, MCOL, E0, E1, TCOL, TMPC, Q0, Q1, R8 = [col("cf", j) for j in range(9)]
 CMC = [col("cf", 10 + t) for t in range(RO)]
 KAP = [col("cf", 14 + t) for t in range(RO)]
 KT = [col("cf", 18 + t) for t in range(RO)]
-IDN, NIDN, BK, BKN, WB, TB = [v(x, 0, 128) for x in ("idn", "nidn", "bk", "bkn", "wb", "tb")]
+IDN, NIDN, BK, BKN, WB, WL, TB = [v(x, 0, 128) for x in ("idn", "nidn", "bk", "bkn", "wb", "wl", "tb")]
 
 
 def abase(t):
@@ -317,35 +321,44 @@ def setup():
     dma("S", v("wtb", 0, 2), v("wt", 0, 2))
     dma("S", v("hki", 0, 2), v("hk", 0, 2))
     dma("S", v("thi", 0, 2), v("th", 0, 2))
-    dma("Y", v("W", XOFF, AOFF), v("gn", 0, 4096))
-    dma("Y", v("Mo", 0, 2048), v("mh", 0, 2048))
-    dma("Y", v("W", AOFF, AOFF + 4096), v("ar", 0, 4096))
-    dma("Y", v("W", AOFF + 4096, AOFF + AS), v("ar", 0, 32))
-    dma("Y", v("W", abase(1), abase(1) + 4096), v("ar", 0, 4096))
+    last = []
+    for x in CFG["loads"]:
+        if x == "g":
+            last = [dma("Y", v("W", XOFF, AOFF), v("gn", 0, 4096), last)]
+        if x == "m":
+            last = [dma("Y", v("Mo", 0, 2048), v("mh", 0, 2048), last, True)]
+        if x == "a":
+            last = [dma("Y", v("W", AOFF + 4096, AOFF + AS), v("ar", 0, 32), last, True)]
+            last = [dma("Y", v("W", AOFF, AOFF + 4096), v("ar", 0, 4096), last, True)]
+    if not CFG["late"]:
+        dma("Y", v("W", abase(1), abase(1) + 4096), v("ar", 0, 4096), last, True)
     memset(v("ones", 0, 128), 1.0)
     asel(v("blk0", 0, 128), v("ones", 0, 128), [[-16, 8], [0, 16]], ALU.is_ge, 0, 1)
     asel(v("blk", 0, 128), v("blk0", 0, 128), [[16, 8], [0, 16]], ALU.is_ge, 15, -1)
+    iota(v("wi", 0, 128), [[0, 8], [2, 16]], 1, 0)
     iota(v("ci", 0, 1), [[0, 1]], 0, 1)
     asel(IDN, v("ones", 0, 128), [[-1, 128]], ALU.is_equal, 0, 1)
     iota(v("ai", 0, 288), [[1, 9], [4, 2], [0, 16]], 0, 0)
-    iota(v("b0", 0, 64), [[128, 2], [256, 16], [16, 2]], FL + 1024 - 4096, 0)
-    iota(v("c16", 0, 256), [[16, 256]], 0, 0)
+    iota(v("b0", 0, 128), [[32, 4], [128, 2], [256, 16]], XOFF, 0)
+    iota(v("c32", 0, 128), [[32, 128]], 0, 0)
     iota(v("q8", 0, 8), [[1, 4], [4, 2]], 0, 0)
     ts(WB, v("blk", 0, 128), col("wtb", 0), ALU.mult)
+    ts(v("wi", 0, 128), v("wi", 0, 128), col("wtb", 0), ALU.mult)
+    ts(v("wi", 0, 128), v("wi", 0, 128), 255, ALU.bitwise_and)
+    tt(WL, v("wi", 0, 128), v("blk", 0, 128), ALU.mult)
     ts(v("ci", 1, 2), v("ci", 0, 1), 15, ALU.bitwise_and)
     copy(RHO, v("ci", 1, 2))
-    ts(MCOL, v("ci", 1, 2), 2.0, ALU.mult, 1.0, ALU.add)
     ts(R8, v("ci", 1, 2), 8.0, ALU.mult)
-    ts(Q0, v("ci", 1, 2), -float(KU), ALU.mult, float(FL), ALU.add)
-    ts(Q1, v("ci", 1, 2), -float(KU), ALU.mult, float(FL - 16 * KU + 16), ALU.add)
+    ts(Q0, v("ci", 1, 2), float(KU), ALU.mult, -float(MU + 29 * KU), ALU.add)
+    ts(MCOL, v("ci", 1, 2), 12.0, ALU.min)
+    ts(Q1, MCOL, float(KU), ALU.mult, float(16 * KU - MU), ALU.add)
     for t in range(RO):
-        ts(CMC[t], v("ci", 1, 2), -KU / 16.0, ALU.mult, float(3 * KU + 15 * KU // 16 + 1024 + AS * t), ALU.add)
+        ts(CMC[t], v("ci", 1, 2), -float(MU), ALU.mult, float(3 * KU + 15 * MU + abase(t)), ALU.add)
     ts(v("ai", 0, 288), v("ai", 0, 288), 7, ALU.bitwise_and)
     ts(v("t0", 0, 288), v("ai", 0, 288), RHO, ALU.is_lt, Q0, ALU.mult)
-    for s in range(1, 4):
-        ts(v("b0", 64 * s, 64 * s + 64), v("b0", 0, 64), 32.0 * s, ALU.add)
+    ts(v("t0", 0, 288), v("t0", 0, 288), float(29 * KU), ALU.add)
     for t in range(RO - 1):
-        ts(v("ba", 64 * t, 64 * t + 64), v("b0", 0, 64), 32.0 * t + 4096 + AS * t, ALU.add)
+        ts(v("ba", 32 * t, 32 * t + 32), v("b0", 32 * t, 32 * t + 32), float(abase(t) - XOFF), ALU.add)
     copy(v("PF", 0, 2), v("hki", 0, 2))
     copy(v("PF", 2, 4), v("thi", 0, 2))
     copy(v("PF", 4, 6), v("wtb", 0, 2))
@@ -372,10 +385,10 @@ def setup():
     memset(v("m32", 0, 512, 32), 0.0)
     ts(BK, v("blk", 0, 128), BIG, ALU.mult)
     ts(BKN, v("blk", 0, 128), -BIG, ALU.mult)
-    memset(v("cst", 384, 512), float(FL))
     for t in range(RO):
         pr = "PR%d" % t
-        memset(v("cst", 128 * t, 128 * t + 128), 1024.0 - 4096.0 * (t + 2))
+        if t < RO - 1:
+            memset(v("cst", 64 * t, 64 * t + 64), float(XOFF - 4096 * (t + 1)))
         ts(v("wj", 128 * t, 128 * t + 128), v("blk", 0, 128), col(pr, 5), ALU.mult)
         ts(KT[t], col(pr, 1), 895.5, ALU.is_ge, -65536.0, ALU.mult)
         ts(KAP[t], col(pr, 1), 32.0, ALU.mult, KT[t], ALU.add)
@@ -433,46 +446,56 @@ def sums(out, first, by_m):
         mm([(out, zsel("zs", 0, m), by_m[m]) for m in range(k, 16)], False, True)
 
 
+def places(lst, first, w0):
+    for q in range(2):
+        ts(sub(lst, q, count(lst), 2), first[q], RHO, ALU.add, float(16 * q - w0), ALU.add)
+
+
 def flanks(t, h):
     n = NG[h]
     nb = n // 16
     ps, pa = "PS%d" % h, "PA%d" % h
     w0 = tbase(t - 1, h)
     awin = v("W", abase(t), abase(t) + AS)
-    si, u, uu, p, lq = [slot("I", h, k) for k in range(5)]
+    u, uu, p, lq, si, sl = [slot("I", h, k) for k in range(1, 7)]
     if t == 0:
         def x0(r, b):
             lo = XOFF + 32 * gene0(h, b) + place(r, h, b)
             return v("W", lo, lo + 15 * 256 + 1, 256)
-        mm([(v(ps, 16 * b, 16 * b + 16), WB, x0(0, b)) for b in range(nb)])
-        copy(si, v(ps, 0, n))
+        mm([(v(ps, n * j + 16 * b, n * j + 16 * b + 16), w, x0(0, b)) for j, w in enumerate((WB, WL))
+            for b in range(nb)])
+        copy(slot("I", h, 5, 2), v(ps, 0, 2 * n))
         mm([(v(pa, n * r + 16 * b, n * r + 16 * b + 16), IDN, x0(r, b)) for r in range(RO) for b in range(nb)])
         act(slot("X", h, 0, 3), v(pa, 0, 3 * n), ACT.Identity)
-        beta = v("b0", 64 * CH[h][0], 64 * CH[h][0] + 2 * n)
-    else:
-        beta = own(h, 2, 2)
+    beta = v("b0", 32 * CH[h][0], 32 * CH[h][0] + n) if t == 0 else slot("F", h, 0)
     xa = slot("X", h, (0, 3, 5)[t])
     at = 32 * place(t, h, 0)
-    la, xo, f3, key = slot("F", h, 3), slot("F", h, 4), slot("F", h, 5), slot("F", h, 6)
+    la, xo, f3, key = own(h, 3), slot("F", h, 4), slot("F", h, 5), slot("F", h, 6)
+    ts(lq, sl, 4, ALU.arith_shift_right, 15, ALU.bitwise_and)
     ts(u, si, 4095, ALU.bitwise_and)
+    if CFG["ba"]:
+        tt(own(h, 2), beta, v("ai", at, at + n), ALU.add)
+        tt(xo, lq, own(h, 2), ALU.add)
+    tt(la, lq, v("ai", at, at + n), ALU.add)
+    if not CFG["ba"]:
+        tt(xo, beta, la, ALU.add)
+    ts(slot("U", h, 2), xo, float(4 - w0), ALU.add)
     tt(uu, u, u, ALU.mult)
-    ts(lq, u, MCOL, ALU.mult)
     ts(own(h, 0), u, col("PF", 0), ALU.mult)
     ts(uu, uu, 5, ALU.arith_shift_right)
-    ts(lq, lq, 4, ALU.arith_shift_right, 15, ALU.bitwise_and)
     tt(uu, uu, own(h, 0), ALU.add)
-    tt(la, lq, v("ai", at, at + n), ALU.add)
     ts(p, uu, 4095, ALU.bitwise_and)
-    tt(xo, la, sub(beta, 0, 2 * n, 2), ALU.add)
     copy(slot("U", h, 0), p)
-    ts(slot("U", h, 2), xo, float(AOFF - FL - 1024 - w0 + 4), ALU.add)
     tt(f3, p, lq, ALU.add)
     ts(slot("U", h, 1), f3, 4.0, ALU.add)
     ts(own(h, 1), la, float(KU - 1), ALU.mult, CMC[t], ALU.add)
     tt(key, f3, own(h, 1), ALU.add)
     if t < RO - 1:
-        mm([(v(ps, n, 2 * n), WB, slot("X", h, (1, 4)[t]))])
-        act(slot("F", h, 2), v(ps, n, 2 * n), ACT.Identity, bias=float(2 ** 21))
+        mm([(v(ps, n * j, n * j + n), w, slot("X", h, (1, 4)[t])) for j, w in enumerate((WB, WL))])
+        act(slot("F", h, 2, 2), v(ps, 0, 2 * n), ACT.Identity, bias=float(2 ** 21))
+    keep = slot("F", h, 10, 2)
+    tt(sub(keep, 0, n), beta, v("t0", at, at + n), ALU.add)
+    ts(sub(keep, n, 2 * n), beta, Q1, ALU.add)
     G, E, D = [slot(x, h, 0, 16) for x in "GED"]
     AA, AB = slot("A", h, 0, 16), slot("A", h, 16, 16)
     gather(E, v("W", w0, AOFF), slot("U", h, 2))
@@ -498,12 +521,16 @@ def flanks(t, h):
     scan(s1, v("m16", 0, n), tr)
     scan((s2[0], s2[1], s2[2], -1), v("m16", 0, n), (s1[0], s1[1], s1[2], -1))
     vtr(best, s2)
-    z, f = slot("I", h, 5, 2), slot("F", h, 10, 2)
-    tt(sub(z, 0, 2 * n, 2), best, v("t0", at, at + n), ALU.add)
-    ts(sub(z, 1, 2 * n, 2), best, Q1, ALU.add)
-    ts(z, z, FL + KU // 16 - 1, ALU.bitwise_and)
-    tt(f, z, beta, ALU.max)
-    ts(slot("U", h, 4, 2), f, RHO, ALU.add, float(AOFF - FL - 1024 - w0), ALU.add)
+    for q in range(2):
+        z = slot("I", h, 5 + q)
+        tt(z, best, sub(keep, n * q, n * q + n), ALU.max)
+        if n > 32:
+            ts(z, z, MU - 1, ALU.bitwise_and)
+    if n == 32:
+        ts(slot("I", h, 5, 2), slot("I", h, 5, 2), MU - 1, ALU.bitwise_and)
+    places(slot("U", h, 4, 2), [slot("I", h, 5), slot("I", h, 6)], w0)
+    if CFG["late"] and t == 0 and h == CFG["order"][0][0]:
+        dma("Y", v("W", abase(1), abase(1) + 4096), v("ar", 0, 4096), [len(OPS) - 1])
     t0 = tbase(t, h)
     for lo, hi in pieces(32 * n):
         move(v("W", t0 + lo, t0 + hi), ind(v("W", w0, abase(t) + AS), sub(slot("U", h, 4, 2), lo // 16, hi // 16)))
@@ -539,29 +566,25 @@ def verdict(t, h):
     def new(r, b):
         lo = t0 + 512 * b + place(r, h, b)
         return v("W", lo, lo + 15 * 32 + 1, 32)
-    cb, sn = v(pa, 0, 2 * n), v(pa, 2 * n, 3 * n)
-    c0 = (t0 % 4096) // 16
-    pre = [(cb, IDN, v("c16", c0, c0 + 2 * n)), (cb, IDN, v("cst", 128 * t, 128 * t + 2 * n)),
-           (cb, IDN, v("cst", 384, 384 + 2 * n))]
-    post = [(sub(cb, q, 2 * n, 2), BK, hit) for q in range(2)]
+    cb, sn = v(pa, 0, n), v(pa, n, 3 * n)
+    c0 = (t0 % 4096) // 32
+    pre = [(cb, IDN, v("c32", c0, c0 + n))]
+    post = [(cb, BK, hit)]
     if t < RO - 1:
-        pre += [(sub(sn, 16 * b, 16 * b + 16), WB, new(t + 1, b)) for b in range(nb)]
-        post += [(sn, BK, hit)]
+        pre += [(cb, IDN, v("cst", 64 * t, 64 * t + n))]
+        pre += [(sub(sn, n * j + 16 * b, n * j + 16 * b + 16), w, new(t + 1, b))
+                for j, w in enumerate((WB, WL)) for b in range(nb)]
+        post += [(sub(sn, n * j, n * j + n), BK, hit) for j in range(2)]
     mm(pre, True, False)
     mm(post, False, True)
-    beta = v("b0", 64 * s0, 64 * s0 + 2 * n) if t == 0 else slot("F", h, 0, 2)
+    beta = v("b0", 32 * s0, 32 * s0 + n) if t == 0 else slot("F", h, 0)
     if t < RO - 1:
         if s0 <= t < s0 + CH[h][1]:
-            ta, lst = v("F%d" % h, 12 * n, 12 * n + 64), v("U%d" % h, 6 * n, 6 * n + 64)
-            tt(ta, sub(cb, 64 * (t - s0), 64 * (t - s0) + 64), v("ba", 64 * t, 64 * t + 64), ALU.min)
-            ts(lst, ta, RHO, ALU.add, float(AOFF - FL - 1024 - t0), ALU.add)
-        tt(slot("I", h, 0), sn, slot("F", h, 2), ALU.min)
-        if OWN:
-            tt(own(h, 2, 2), beta, cb, ALU.min)
-            if t == 0:
-                tt(slot("F", h, 0, 2), beta, cb, ALU.min)
-        else:
-            tt(own(h, 2, 2), beta if t == 0 else own(h, 2, 2), cb, ALU.min)
+            ta, lst = v("F%d" % h, 12 * n, 12 * n + 32), v("U%d" % h, 6 * n, 6 * n + 64)
+            tt(ta, sub(cb, 32 * (t - s0), 32 * (t - s0) + 32), v("ba", 32 * t, 32 * t + 32), ALU.min)
+            places(lst, [ta, ta], t0)
+        tt(slot("I", h, 5, 2), sn, slot("F", h, 2, 2), ALU.min)
+        tt(slot("F", h, 0), beta, cb, ALU.min)
         if s0 <= t < s0 + CH[h][1]:
             archive_write(t, v("W", t0, abase(t) + AS), lst)
         k = RO - 1 - t
@@ -573,18 +596,16 @@ def verdict(t, h):
         tt(sel, old, lo, ALU.min)
         tt(sel, sel, hi, ALU.max)
     else:
-        f, lst = slot("F", h, 10, 2), slot("U", h, 8, 2)
-        if OWN:
-            copy(slot("F", h, 0, 2), own(h, 2, 2))
-        tt(f, slot("F", h, 0, 2) if OWN else own(h, 2, 2), cb, ALU.min)
-        ts(lst, f, RHO, ALU.add, float(AOFF - FL - 1024 - t0), ALU.add)
+        lst = slot("U", h, 8, 2)
+        tt(beta, beta, cb, ALU.min)
+        places(lst, [beta, beta], t0)
         k = 16 // CFG["ypiece"]
         for r0 in range(0, 16, k):
             for b in range(nb):
                 c = 32 * gene0(h, b)
                 part = v("SO%d" % h, 512 * b + 32 * r0, 512 * b + 32 * (r0 + k))
                 move(part, ind(v("W", t0, AOFF), sub(lst, 32 * b + 2 * r0, 32 * b + 2 * r0 + 2 * k)))
-                move(rows("Y", r0, r0 + k, c, c + 32), part)
+                move(rows("Y", r0, r0 + k, c, c + 32), part, CFG["gy"])
             if h == CFG["order"][t][-1]:
                 dma("Y", v("y", 256 * r0, 256 * (r0 + k)), rows("Y", r0, r0 + k, 0, 256))
 
@@ -636,7 +657,7 @@ def build():
             verdict(t, h)
     seen = {}
     for o in OPS:
-        dep = dict((d, False) for d in o["after"])
+        dep = dict([(d, False) for d in o["after"]] + [(d, True) for d in o.get("wait", [])])
         acc = [(x, cols(x), False) for x in o["r"]] + [(x, cols(x), True) for x in o["w"]]
         for x, m, wr in acc:
             ps = where(x) == "psum"
@@ -678,14 +699,8 @@ def priorities(M, cost):
             for o in OPS]
 
 
-def nudge(prio, seed):
-    s = (seed * 1103515245 + 12345) % (1 << 31)
-    a = (s >> 8) % len(prio)
-    s = (s * 1103515245 + 12345) % (1 << 31)
-    k = (1, 2, 4, 10, 30, 60)[(s >> 8) % 6]
-    s = (s * 1103515245 + 12345) % (1 << 31)
-    d = ((s >> 8) % 2001 - 1000) * 3.0
-    return prio[:a] + [x + d for x in prio[a:a + k]] + prio[a + k:]
+def follows(d, o):
+    return d["kind"] == o["kind"] and d["kind"] in "dr" and not o["dep"][d["id"]]
 
 
 def occupy(M, o, e, t, c, st):
@@ -735,7 +750,7 @@ def schedule(prio, M, cost):
         for j in o["succ"]:
             r = ready[j]
             for q in r:
-                if o["kind"] == "r" and OPS[j]["kind"] == "r":
+                if follows(o, OPS[j]):
                     at = free[e]
                 elif not OPS[j]["dep"][pick]:
                     at = fin[pick]
@@ -749,12 +764,143 @@ def schedule(prio, M, cost):
     return max(fin), order, beg, fin
 
 
+QS = "VSPGYX"
+
+
+def improve(M, cost, order, beg, moves, seed, heat):
+    N = len(OPS)
+    real, loose, pred, succ, above = [], [], [], [set() for o in OPS], []
+    for o in OPS:
+        cover, mine = 0, []
+        for d in sorted(o["dep"], reverse=True):
+            if not cover >> d & 1:
+                mine.append(d)
+                if o["dep"][d]:
+                    cover |= above[d]
+        above.append(cover | sum(1 << d for d in o["dep"] if o["dep"][d] and not cover >> d & 1))
+        real.append([d for d in mine if o["dep"][d]])
+        loose.append([d for d in mine if not o["dep"][d] and not follows(OPS[d], o)])
+        pred.append(set(mine))
+        for d in mine:
+            succ[d].add(o["id"])
+    same, cross = M["same"], M["cross"]
+    plain = [o["kind"] in "cx" for o in OPS]
+    cst = [[c.get(e, 0.0) for e in QS] for c in cost]
+    tail = [0.0] * N
+    for i in range(N - 1, -1, -1):
+        tail[i] += min(cost[i].values()) if plain[i] else 0.0
+        for d in real[i]:
+            tail[d] = max(tail[d], tail[i] + min(same, cross))
+        for d in loose[i]:
+            tail[d] = max(tail[d], tail[i])
+    eng = [0] * N
+    for e in order:
+        for i in order[e]:
+            eng[i] = QS.index(e)
+    lst, seen = [], set()
+
+    def put(i):
+        if i not in seen:
+            seen.add(i)
+            for d in sorted(pred[i]):
+                put(d)
+            lst.append(i)
+    for i in sorted(range(N), key=lambda i: (beg[i], i)):
+        put(i)
+    alts = [[QS.index(e) for e in sorted(o["alt"])] for o in OPS]
+
+    def run(p0, limit, fin, why, snaps):
+        k = p0 >> 4
+        free, last, st, top = [x[:] for x in snaps[k]]
+        top = top[0]
+        for p in range(k << 4, N):
+            if not p & 15:
+                snaps[p >> 4] = (free[:], last[:], st[:], [top])
+            i = lst[p]
+            e = eng[i]
+            t, w = free[e], last[e]
+            for d in real[i]:
+                a = fin[d] + (same if eng[d] == e else cross)
+                if a > t:
+                    t, w = a, d
+            for d in loose[i]:
+                if fin[d] > t:
+                    t, w = fin[d], d
+            if t + tail[i] > limit:
+                return None
+            why[i], last[e] = w, i
+            if plain[i]:
+                t += cst[i][e]
+                free[e] = t
+            else:
+                free[e], t = occupy(M, OPS[i], e, t, cst[i][e], st)
+            fin[i] = t
+            if t > top:
+                top = t
+        return top if top <= limit else None
+
+    def longest(fin, why):
+        i, way = fin.index(max(fin)), []
+        while i >= 0:
+            way.append(i)
+            i = why[i]
+        return way
+    fin, why = [0.0] * N, [-1] * N
+    snaps = [([0.0] * 6, [-1] * 6, [0.0, 0.0], [0.0])] * (N // 16 + 1)
+    cur = run(0, 1e18, fin, why, snaps)
+    way = longest(fin, why)
+    best = (cur, lst[:], eng[:])
+    s = seed
+    for it in range(moves):
+        r = []
+        for k in range(5):
+            s = (s * 1103515245 + 12345) & 0x7FFFFFFF
+            r.append((s >> 4) / float(1 << 27))
+        if r[0] < 0.8:
+            i = way[int(r[1] * len(way))]
+            p = lst.index(i)
+        else:
+            p = int(r[1] * N)
+            i = lst[p]
+        e = old = eng[i]
+        if r[2] < 0.35:
+            e = alts[i][int(r[2] / 0.35 * len(alts[i]))]
+        k = int(-math.log(1.0 - r[3]) / 0.45) + (e == old)
+        q = p
+        if s >> 12 & 1:
+            stop = pred[i]
+            while q > 0 and k and lst[q - 1] not in stop:
+                q -= 1
+                k -= eng[lst[q]] == e
+        else:
+            stop = succ[i]
+            while q < N - 1 and k and lst[q + 1] not in stop:
+                q += 1
+                k -= eng[lst[q]] == e
+        if q == p and e == old:
+            continue
+        del lst[p]
+        lst.insert(q, i)
+        eng[i] = e
+        f2, w2, s2 = fin[:], why[:], snaps[:]
+        warm = heat[0] * (heat[1] / heat[0]) ** (it / float(moves))
+        c = run(min(p, q), cur - warm * math.log(1.0 - r[4]), f2, w2, s2)
+        if c is None:
+            del lst[q]
+            lst.insert(p, i)
+            eng[i] = old
+        else:
+            cur, fin, why, snaps = c, f2, w2, s2
+            way = longest(fin, why)
+            if cur < best[0]:
+                best = (cur, lst[:], eng[:])
+    return best[0], dict((e, [i for i in best[1] if QS[best[2][i]] == e]) for e in QS)
+
+
 def plan():
     cost = price(MODEL)
-    prio = priorities(MODEL, cost)
-    for s in CFG["steps"]:
-        prio = nudge(prio, s)
-    return schedule(prio, MODEL, cost)
+    end, order, beg, fin = schedule(priorities(MODEL, cost), MODEL, cost)
+    return improve(MODEL, cost, order, beg, CFG["moves"], CFG["seed"], CFG["heat"])
 
 
 build()

import math

from concourse.bass import DstId, RemoteDMATransfer
from concourse.mybir import AluOpType, ActivationFunctionType

ALU = AluOpType
ACT = ActivationFunctionType

NR = 4
RO = 3
XOFF, AOFF, AS = 12288, 16384, 4128
WEND = AOFF + RO * AS
BIG = float(2 ** 22)
ES = float(2 ** 25)
MU = 2 ** 15
KU = 17 * MU

CFG = {"chunks": [(0, 1), (1, 1), (2, 2)], "order": [[0, 1, 2], [1, 0, 2], [2, 1, 0]], "piece": 512, "both": False,
       "arch": "tmp", "ba": True, "gy": True, "gcopy": True, "ypiece": 4, "late": True, "loads": "gma",
       "bias": 2000.0, "delta": 60.0, "pen": 6000.0, "slack": 100.0, "moves": 250000, "seed": 1, "heat": (40.0, 2.0)}
MODEL = {"cy": 0.85, "g": 1.56, "sc": 3.8, "pcy": 0.45, "same": 220.0, "cross": 260.0, "issue": 60.0, "dma": 1100.0,
         "rate": 420.0, "riss": 700.0, "rfirst": 2500.0, "rem": 1800.0, "rrate": 70.0}

CH = CFG["chunks"]
NG = [32 * w for s, w in CH]
OWN = sum(w + 1 for s, w in CH) < 8

SCRATCH = {}
SEMAPHORES = ["cV", "cS", "cP", "cG", "sent"]
for _dt, _list in [
    ("bfloat16", [("W", WEND), ("Mo", 2048), ("M0", 2048), ("M1", 2048), ("M2", 2048), ("wtb", 8),
                  ("ones", 128), ("blk0", 128), ("blk", 128), ("idn", 128), ("nidn", 128), ("bk", 128), ("bkn", 128),
                  ("wb", 128), ("tb", 128), ("wj", 384), ("zs", 144), ("zw", 288), ("wl", 128), ("c32", 128), ("cst", 128),
                  ("m32", 1024), ("tmp", 1024), ("zc0", 128), ("zc1", 128), ("zl0", 128), ("zl1", 128), ("zl2", 128)]),
    ("float32", [("PF", 8), ("PR0", 8), ("PR1", 8), ("PR2", 8), ("b0", 128), ("ba", 64), ("t0", 288), ("cf", 32),
                 ("m16", 64), ("q8", 8), ("sf", 8)]),
    ("int32", [("hki", 4), ("thi", 4), ("ai", 288), ("wi", 128), ("ci", 8), ("si", 16)]),
    ("uint16", [("so0", 8), ("so1", 8), ("sl0", 8), ("sl1", 8), ("sl2", 8)]),
]:
    for _nm, _cols in _list:
        SCRATCH[_nm] = ("sbuf", [128, _cols], _dt)
SCRATCH["Y"] = ("sbuf", [128, 16, 256], "bfloat16")
for _h, _n in enumerate(NG):
    for _nm, _cols, _dt in [
        ("I", 7, "int32"), ("F", 18, "float32"), ("U", 10, "uint16"), ("X", 7, "bfloat16"), ("G", 16, "bfloat16"),
        ("E", 16, "bfloat16"), ("D", 16, "bfloat16"), ("A", 32, "bfloat16"), ("SO", 32, "bfloat16"),
    ]:
        SCRATCH["%s%d" % (_nm, _h)] = ("sbuf", [128, _cols * _n], _dt)
    for _nm in ["PS", "PA", "PB"][:1 + CH[_h][1]]:
        SCRATCH["%s%d" % (_nm, _h)] = ("psum", [128, 512], "float32")
if OWN:
    SCRATCH["PV"] = ("psum", [128, 512], "float32")
INPUTS = ("gn", "ar", "mh", "wt", "hk", "th", "y")


def v(name, lo, hi, step=1):
    return (name, lo, hi, step)


def rows(name, r0, r1, lo, hi):
    return (name, r0, r1, lo, hi)


def sub(d, lo, hi, step=1):
    return (d[0], d[1] + lo * d[3], min(d[2], d[1] + hi * d[3]), d[3] * step)


def cols(d):
    if len(d) == 5:
        row = SCRATCH[d[0]][1][2]
        return sum(((1 << (d[4] - d[3])) - 1) << (row * r + d[3]) for r in range(d[1], d[2]))
    if d[3] in (1, -1):
        return ((1 << (d[2] - d[1])) - 1) << d[1]
    return sum(1 << c for c in range(d[1], d[2], d[3]))


def count(d):
    if len(d) == 5:
        return (d[2] - d[1]) * (d[4] - d[3])
    return len(range(d[1], d[2], abs(d[3])))


def ap(T, d):
    t = T[d[0]]
    if len(d) == 5:
        return t[:, d[1]:d[2], d[3]:d[4]]
    if d[3] == -1:
        return t[:, d[2] - 1:d[1] - 1:-1]
    return t[:, d[1]:d[2]] if d[3] == 1 else t[:, d[1]:d[2]:d[3]]


def arg(T, x):
    if not isinstance(x, tuple):
        return x
    return ap(T, x[1]).indirect(ap(T, x[2])) if x[0] == "ind" else ap(T, x)


def ind(win, off):
    return ("ind", win, off)


def where(d):
    return SCRATCH[d[0]][0] if d[0] in SCRATCH else "hbm"


OPS = []
TAG = [None]
ARR = {}


def add(alts, reads, writes, kind="c", sem=None, after=()):
    OPS.append({"alt": alts, "eng": sorted(alts)[0] if len(alts) == 1 else "F", "r": reads, "w": writes,
                "kind": kind, "sem": sem, "after": list(after), "id": len(OPS), "tag": TAG[0]})
    return len(OPS) - 1


def vcost(out, ins, both=False):
    if out[0] == "ind":
        return (50, 0, 0, count(ins[0]), 0)
    if ins and ins[0][0] == "ind":
        return (50, 0, count(out), 0, 0)
    if both:
        c = 2.0 if all(where(x) == "sbuf" for x in ins) else 1.0
    else:
        c = 0.5 if all(SCRATCH[x[0]][2] in ("bfloat16", "uint16") for x in ins + [out]) else 1.0
    return (0, max(64.0, c * count(out)), 0, 0, 0)


def rw(out, ins):
    r = []
    for x in ins:
        if isinstance(x, tuple):
            r += [x[1], x[2]] if x[0] == "ind" else [x]
    if out[0] == "ind":
        return r + [out[2]], [out[1]]
    return r, [out]


def v_copy(out, in_):
    return (lambda c: c["g"].vector.tensor_copy(arg(c["T"], out), arg(c["T"], in_)), vcost(out, [in_]))


def s_act(out, in_, func, bias=0.0, scale=1.0):
    cost = (65, 0, count(out), 0, 0) if in_[0] == "ind" else (0, max(64.0, count(out)), 0, 0, 0)
    return (lambda c: c["g"].scalar.activation(arg(c["T"], out), arg(c["T"], in_), func, bias=arg(c["T"], bias),
                                               scale=scale), cost)


def g_sel(out, in_, pattern, op, base, cm):
    return (lambda c: c["g"].affine_select(arg(c["T"], out), arg(c["T"], in_), pattern, op, 0.0, base, cm),
            (170, 2 * count(out), 0, 0, 0))


def copy(out, in_):
    return add({"V": v_copy(out, in_)}, *rw(out, [in_]))


def move(out, in_, pool=False):
    alts = {"V": v_copy(out, in_), "S": s_act(out, in_, ACT.Identity)}
    if pool:
        alts["G"] = g_sel(out, in_, [[0, count(out)]], ALU.is_ge, 0, 0)
    return add(alts, *rw(out, [in_]))


def act(out, in_, func, bias=0.0, scale=1.0):
    return add({"S": s_act(out, in_, func, bias, scale)}, *rw(out, [in_, bias]))


def tt(out, a, b, op):
    return add({"V": (lambda c: c["g"].vector.tensor_tensor(arg(c["T"], out), arg(c["T"], a), arg(c["T"], b), op),
                      vcost(out, [a, b], True))}, *rw(out, [a, b]))


def ts(out, a, s1, op0, s2=None, op1=None):
    def fn(c):
        T = c["T"]
        if op1 is None:
            return c["g"].vector.tensor_scalar(arg(T, out), arg(T, a), arg(T, s1), None, op0)
        return c["g"].vector.tensor_scalar(arg(T, out), arg(T, a), arg(T, s1), arg(T, s2), op0, op1)
    return add({"V": (fn, vcost(out, [a]))}, *rw(out, [a, s1, s2]))


def memset(out, val):
    return add({"V": (lambda c: c["g"].vector.memset(arg(c["T"], out), val), vcost(out, []))}, [], [out])


def scan(out, mask, data):
    return add({"V": (lambda c: c["g"].vector.tensor_tensor_scan(arg(c["T"], out), arg(c["T"], mask),
                                                                 arg(c["T"], data), 0.0, ALU.mult, ALU.max),
                      vcost(out, [mask, data]))}, [mask, data], [out])


def vtr(out, in_):
    return add({"V": (lambda c: c["g"].vector.transpose(arg(c["T"], out), arg(c["T"], in_)), vcost(out, [in_]))},
               [in_], [out])


def mm(items, start=True, stop=True):
    def fn(c):
        T = c["T"]
        last = None
        for i, (o, l, x) in enumerate(items):
            last = c["g"].tensor.matmul(arg(T, o), arg(T, l), arg(T, x), start and i == 0,
                                        stop and i == len(items) - 1)
        return last
    return add({"P": (fn, (0, 0, 0, 0, sum(max(64, count(x)) for o, l, x in items)))},
               [l for o, l, x in items] + [x for o, l, x in items], [o for o, l, x in items])


def iota(out, pattern, base, cm):
    def fn(c):
        if SCRATCH[out[0]][2] == "int32":
            return c["g"].iota(arg(c["T"], out), pattern, base, cm)
        return c["g"].iota(arg(c["T"], out), pattern, base, cm, allow_small_or_imprecise_dtypes=True)
    return add({"G": (fn, (130, 2 * count(out), 0, 0, 0))}, [], [out])


def asel(out, in_, pattern, op, base, cm):
    return add({"G": g_sel(out, in_, pattern, op, base, cm)}, [in_], [out])


def dma(eng, out, in_, after=(), behind=False):
    sem = "d%d" % len(SEMAPHORES)
    SEMAPHORES.append(sem)
    side = in_ if out[0] in INPUTS else out
    nbytes = 128 * count(side) * (2 if SCRATCH[side[0]][2] == "bfloat16" else 4)

    def fn(c):
        q = c["g"].sync if eng == "Y" else c["g"].scalar
        return q.dma_start(arg(c["T"], out), arg(c["T"], in_))
    i = add({eng: (fn, nbytes)}, [] if in_[0] in INPUTS else [in_], [] if out[0] in INPUTS else [out], "d", sem,
            after=after if behind else ())
    OPS[i]["wait"] = [] if behind else list(after)
    return i


def share(c, backs):
    topo, me = c["topo"], c["core"]
    dsts = [c["T"].cores[(c["rank"] - b) % NR] for b in backs]
    used = {}
    out = {}
    order = sorted(range(len(dsts)), key=lambda i: len(topo.engines(me, dsts[i])))
    narrow = [i for i in order if len(topo.engines(me, dsts[i])) == len(topo.engines(me, dsts[order[0]]))]
    for i in order:
        left = [e for e in topo.engines(me, dsts[i]) if e not in used]
        k = len(left) // len([j for j in narrow if j not in out]) if i in narrow else len(left)
        p = 1
        while 2 * p <= k:
            p *= 2
        m = 0
        for e in left[:p]:
            used[e] = 1
            m |= 1 << e
        out[i] = (dsts[i], m, p)
    return [out[i] for i in range(len(dsts))]


def send(src, dests, nbytes, after=()):
    backs = [b for b, d, s in dests]

    def fn(c):
        T, topo = c["T"], c["topo"]
        trs = []
        for (core, m, p), (b, d, s) in zip(share(c, backs), dests):
            assert topo.may_write(c["core"], core)
            rid, pid, se = topo.addr(core)
            trs.append(RemoteDMATransfer(dst_ids=[DstId(rid=rid, pnc=pid)], dma_engine_mask=m, remote_sem=T.sem[s],
                                         src=arg(T, src), dst=arg(T, d)))
            c["sent"][0] += p
        c["g"].remote_dma_fused(trs, local_sem=T.sem.sent)
        return None
    return add({"G": (fn, nbytes)}, [src], [], "r", after=after)


def arrive(sem, writes, calls, sends):
    SEMAPHORES.append(sem)
    ARR[sem] = calls
    return add({"X": (None, 0)}, [], writes, "x", sem, after=sends)


def arrival_count(c, sem):
    tot = 0
    for back, backs in ARR[sem]:
        r = (c["rank"] + back) % NR
        other = {"topo": c["topo"], "T": c["T"], "rank": r, "core": c["T"].cores[r]}
        tot += share(other, backs)[backs.index(back)][2]
    return tot


def col(name, j):
    return v(name, j, j + 1)


RHO, MCOL, E0, E1, TCOL, TMPC, Q0, Q1, R8 = [col("cf", j) for j in range(9)]
CMC = [col("cf", 10 + t) for t in range(RO)]
KAP = [col("cf", 14 + t) for t in range(RO)]
KT = [col("cf", 18 + t) for t in range(RO)]
IDN, NIDN, BK, BKN, WB, WL, TB = [v(x, 0, 128) for x in ("idn", "nidn", "bk", "bkn", "wb", "wl", "tb")]


def abase(t):
    return AOFF + AS * t


def tbase(t, h):
    if t < 0:
        return XOFF
    o = CFG["order"][t]
    return XOFF - 4096 * t - 32 * sum(NG[k] for k in o[:o.index(h) + 1])


def place(t, h, blk):
    return (CH[h][0] + blk // 2 + 4 * (blk % 2) + 3 * t) % 8


def gene0(h, blk):
    return CH[h][0] + blk // 2 + 4 * (blk % 2)


def setup():
    dma("S", v("wtb", 0, 2), v("wt", 0, 2))
    dma("S", v("hki", 0, 2), v("hk", 0, 2))
    dma("S", v("thi", 0, 2), v("th", 0, 2))
    last = []
    for x in CFG["loads"]:
        if x == "g":
            last = [dma("Y", v("W", XOFF, AOFF), v("gn", 0, 4096), last)]
        if x == "m":
            last = [dma("Y", v("Mo", 0, 2048), v("mh", 0, 2048), last, True)]
        if x == "a":
            last = [dma("Y", v("W", AOFF + 4096, AOFF + AS), v("ar", 0, 32), last, True)]
            last = [dma("Y", v("W", AOFF, AOFF + 4096), v("ar", 0, 4096), last, True)]
    if not CFG["late"]:
        dma("Y", v("W", abase(1), abase(1) + 4096), v("ar", 0, 4096), last, True)
    memset(v("ones", 0, 128), 1.0)
    asel(v("blk0", 0, 128), v("ones", 0, 128), [[-16, 8], [0, 16]], ALU.is_ge, 0, 1)
    asel(v("blk", 0, 128), v("blk0", 0, 128), [[16, 8], [0, 16]], ALU.is_ge, 15, -1)
    iota(v("wi", 0, 128), [[0, 8], [2, 16]], 1, 0)
    iota(v("ci", 0, 1), [[0, 1]], 0, 1)
    asel(IDN, v("ones", 0, 128), [[-1, 128]], ALU.is_equal, 0, 1)
    iota(v("ai", 0, 288), [[1, 9], [4, 2], [0, 16]], 0, 0)
    iota(v("b0", 0, 128), [[32, 4], [128, 2], [256, 16]], XOFF, 0)
    iota(v("c32", 0, 128), [[32, 128]], 0, 0)
    iota(v("q8", 0, 8), [[1, 4], [4, 2]], 0, 0)
    ts(WB, v("blk", 0, 128), col("wtb", 0), ALU.mult)
    ts(v("wi", 0, 128), v("wi", 0, 128), col("wtb", 0), ALU.mult)
    ts(v("wi", 0, 128), v("wi", 0, 128), 255, ALU.bitwise_and)
    tt(WL, v("wi", 0, 128), v("blk", 0, 128), ALU.mult)
    ts(v("ci", 1, 2), v("ci", 0, 1), 15, ALU.bitwise_and)
    copy(RHO, v("ci", 1, 2))
    ts(R8, v("ci", 1, 2), 8.0, ALU.mult)
    ts(Q0, v("ci", 1, 2), float(KU), ALU.mult, -float(MU + 29 * KU), ALU.add)
    ts(MCOL, v("ci", 1, 2), 12.0, ALU.min)
    ts(Q1, MCOL, float(KU), ALU.mult, float(16 * KU - MU), ALU.add)
    for t in range(RO):
        ts(CMC[t], v("ci", 1, 2), -float(MU), ALU.mult, float(3 * KU + 15 * MU + abase(t)), ALU.add)
    ts(v("ai", 0, 288), v("ai", 0, 288), 7, ALU.bitwise_and)
    ts(v("t0", 0, 288), v("ai", 0, 288), RHO, ALU.is_lt, Q0, ALU.mult)
    ts(v("t0", 0, 288), v("t0", 0, 288), float(29 * KU), ALU.add)
    for t in range(RO - 1):
        ts(v("ba", 32 * t, 32 * t + 32), v("b0", 32 * t, 32 * t + 32), float(abase(t) - XOFF), ALU.add)
    copy(v("PF", 0, 2), v("hki", 0, 2))
    copy(v("PF", 2, 4), v("thi", 0, 2))
    copy(v("PF", 4, 6), v("wtb", 0, 2))
    s0 = send(v("PF", 0, 6), [(t + 1, v("PR%d" % t, 0, 6), "ap%d" % t) for t in range(RO)], 3072)
    s = s0
    for t in range(RO - 1):
        s = send(v("Mo", 0, 2048), [(t + 1, v("M%d" % t, 0, 2048), "am%d" % t)], 1 << 19, after=[s])
        arrive("ap%d" % t, [v("PR%d" % t, 0, 6)], [(t + 1, [1, 2, 3])], [s0])
        arrive("am%d" % t, [v("M%d" % t, 0, 2048)], [(t + 1, [t + 1])], [s])
    arrive("ap2", [v("PR2", 0, 6)], [(3, [1, 2, 3])], [s0])
    ts(NIDN, IDN, -1.0, ALU.mult)
    memset(v("zs", 0, 144), 0.0)
    ts(v("zs", 15, 128, 16), v("blk", 0, 128, 16), -ES, ALU.mult)
    ts(E0, v("ci", 1, 2), 0.0, ALU.is_equal, ES, ALU.mult)
    ts(E1, v("ci", 1, 2), 1.0, ALU.is_equal, ES, ALU.mult)
    ts(v("ci", 2, 3), v("thi", 0, 1), 8128, ALU.bitwise_and)
    ts(v("ci", 3, 4), v("thi", 0, 1), 63, ALU.bitwise_and)
    ts(TMPC, v("ci", 2, 3), E0, ALU.mult)
    ts(TCOL, v("ci", 3, 4), E1, ALU.mult, TMPC, ALU.add)
    ts(TB, v("blk", 0, 128), TCOL, ALU.mult)
    memset(v("m16", 0, 64), 1.0)
    memset(v("m16", 0, 64, 16), 0.0)
    memset(v("m32", 0, 512), 1.0)
    memset(v("m32", 0, 512, 32), 0.0)
    ts(BK, v("blk", 0, 128), BIG, ALU.mult)
    ts(BKN, v("blk", 0, 128), -BIG, ALU.mult)
    for t in range(RO):
        pr = "PR%d" % t
        if t < RO - 1:
            memset(v("cst", 64 * t, 64 * t + 64), float(XOFF - 4096 * (t + 1)))
        ts(v("wj", 128 * t, 128 * t + 128), v("blk", 0, 128), col(pr, 5), ALU.mult)
        ts(KT[t], col(pr, 1), 895.5, ALU.is_ge, -65536.0, ALU.mult)
        ts(KAP[t], col(pr, 1), 32.0, ALU.mult, KT[t], ALU.add)
    for t in range(RO - 1):
        ts(v("zw", 144 * t, 144 * t + 144), v("zs", 0, 144), col("PR%d" % t, 5), ALU.mult, -128.0 / ES, ALU.mult)


def slot(name, h, k, w=1):
    return v("%s%d" % (name, h), NG[h] * k, NG[h] * (k + w))


def own(h, k, w=1):
    if OWN:
        lo = 4 * sum(NG[:h]) + NG[h] * k
        return v("PV", lo, lo + NG[h] * w)
    return slot("F", h, 14 + k, w)


def pieces(total):
    k = min(CFG["piece"], total)
    return [(lo, lo + k) for lo in range(0, total, k)]


def gather(out, win, lst):
    for lo, hi in pieces(count(out)):
        move(sub(out, lo, hi), ind(win, sub(lst, lo // 16, hi // 16)))


def diffs(h, y, src, dst):
    n = NG[h]
    if n == 32:
        bank = "PA%d" % h
        mm([(v(bank, m, 512, 16), NIDN, y) for m in range(16)], True, False)
        ps = pieces(512)
        for lo, hi in ps:
            mm([(v(bank, lo, hi), IDN, sub(src, lo, hi))], False, hi == 512)
        act(dst, v(bank, 0, 512), ACT.Abs)
        return [sub(dst, m, 512, 16) for m in range(16)]
    for b, bank in enumerate(("PA%d" % h, "PB%d" % h)):
        reg = [v(bank, n * k, n * (k + 1)) for k in range(8)]
        mm([(reg[k], NIDN, y) for k in range(8)], True, False)
        mm([(reg[k], IDN, sub(src, 8 * b + k, 16 * n, 16)) for k in range(8)], False, True)
        act(sub(dst, 512 * b, 512 * b + 512), v(bank, 0, 512), ACT.Abs)
    return [sub(dst, n * m, n * m + n) for m in range(16)]


def zsel(name, base, m):
    return v(name, base + 15 - m, base + 143 - m)


def sums(out, first, by_m):
    k = 16 if count(out) == 32 or by_m[0][3] != 1 else 8
    mm(first + [(out, zsel("zs", 0, m), by_m[m]) for m in range(k)], True, k == 16)
    if k < 16:
        mm([(out, zsel("zs", 0, m), by_m[m]) for m in range(k, 16)], False, True)


def places(lst, first, w0):
    for q in range(2):
        ts(sub(lst, q, count(lst), 2), first[q], RHO, ALU.add, float(16 * q - w0), ALU.add)


def flanks(t, h):
    n = NG[h]
    nb = n // 16
    ps, pa = "PS%d" % h, "PA%d" % h
    w0 = tbase(t - 1, h)
    awin = v("W", abase(t), abase(t) + AS)
    u, uu, p, lq, si, sl = [slot("I", h, k) for k in range(1, 7)]
    if t == 0:
        def x0(r, b):
            lo = XOFF + 32 * gene0(h, b) + place(r, h, b)
            return v("W", lo, lo + 15 * 256 + 1, 256)
        mm([(v(ps, n * j + 16 * b, n * j + 16 * b + 16), w, x0(0, b)) for j, w in enumerate((WB, WL))
            for b in range(nb)])
        copy(slot("I", h, 5, 2), v(ps, 0, 2 * n))
        mm([(v(pa, n * r + 16 * b, n * r + 16 * b + 16), IDN, x0(r, b)) for r in range(RO) for b in range(nb)])
        act(slot("X", h, 0, 3), v(pa, 0, 3 * n), ACT.Identity)
    beta = v("b0", 32 * CH[h][0], 32 * CH[h][0] + n) if t == 0 else slot("F", h, 0)
    xa = slot("X", h, (0, 3, 5)[t])
    at = 32 * place(t, h, 0)
    la, xo, f3, key = own(h, 3), slot("F", h, 4), slot("F", h, 5), slot("F", h, 6)
    ts(lq, sl, 4, ALU.arith_shift_right, 15, ALU.bitwise_and)
    ts(u, si, 4095, ALU.bitwise_and)
    if CFG["ba"]:
        tt(own(h, 2), beta, v("ai", at, at + n), ALU.add)
        tt(xo, lq, own(h, 2), ALU.add)
    tt(la, lq, v("ai", at, at + n), ALU.add)
    if not CFG["ba"]:
        tt(xo, beta, la, ALU.add)
    ts(slot("U", h, 2), xo, float(4 - w0), ALU.add)
    tt(uu, u, u, ALU.mult)
    ts(own(h, 0), u, col("PF", 0), ALU.mult)
    ts(uu, uu, 5, ALU.arith_shift_right)
    tt(uu, uu, own(h, 0), ALU.add)
    ts(p, uu, 4095, ALU.bitwise_and)
    copy(slot("U", h, 0), p)
    tt(f3, p, lq, ALU.add)
    ts(slot("U", h, 1), f3, 4.0, ALU.add)
    ts(own(h, 1), la, float(KU - 1), ALU.mult, CMC[t], ALU.add)
    tt(key, f3, own(h, 1), ALU.add)
    if t < RO - 1:
        mm([(v(ps, n * j, n * j + n), w, slot("X", h, (1, 4)[t])) for j, w in enumerate((WB, WL))])
        act(slot("F", h, 2, 2), v(ps, 0, 2 * n), ACT.Identity, bias=float(2 ** 21))
    keep = slot("F", h, 10, 2)
    tt(sub(keep, 0, n), beta, v("t0", at, at + n), ALU.add)
    ts(sub(keep, n, 2 * n), beta, Q1, ALU.add)
    G, E, D = [slot(x, h, 0, 16) for x in "GED"]
    AA, AB = slot("A", h, 0, 16), slot("A", h, 16, 16)
    gather(E, v("W", w0, AOFF), slot("U", h, 2))
    gather(G, awin, slot("U", h, 0))
    d1 = diffs(h, xa, G, AA)
    both = CFG["both"] and n == 32
    e1, e2 = v(ps, 2 * n, 3 * n), v(ps, 3 * n, 4 * n) if both else v(pa, 0, n)
    if not both:
        sums(e1, [(e1, TB, v("ones", 0, n))], d1)
        tt(key, key, e1, ALU.min)
    for lo, hi in pieces(16 * n):
        tt(sub(D, lo, hi), ind(awin, sub(slot("U", h, 1), lo // 16, hi // 16)), sub(E, lo, hi), ALU.subtract)
        act(sub(AB, lo, hi), sub(D, lo, hi), ACT.Abs)
    if both:
        e12 = v(ps, 2 * n, 4 * n)
        sums(e12, [(e12, TB, v("ones", 0, 2 * n))], [sub(slot("A", h, 0, 32), m, 32 * n, 16) for m in range(16)])
        tt(key, key, e1, ALU.min)
    else:
        sums(e2, [(e2, TB, v("ones", 0, n))], [sub(AB, m, 16 * n, 16) for m in range(16)])
    tr, s1, s2, best = slot("F", h, 7), slot("F", h, 8), slot("F", h, 9), own(h, 1)
    tt(key, key, e2, ALU.min)
    vtr(tr, key)
    scan(s1, v("m16", 0, n), tr)
    scan((s2[0], s2[1], s2[2], -1), v("m16", 0, n), (s1[0], s1[1], s1[2], -1))
    vtr(best, s2)
    for q in range(2):
        z = slot("I", h, 5 + q)
        tt(z, best, sub(keep, n * q, n * q + n), ALU.max)
        if n > 32:
            ts(z, z, MU - 1, ALU.bitwise_and)
    if n == 32:
        ts(slot("I", h, 5, 2), slot("I", h, 5, 2), MU - 1, ALU.bitwise_and)
    places(slot("U", h, 4, 2), [slot("I", h, 5), slot("I", h, 6)], w0)
    if CFG["late"] and t == 0 and h == CFG["order"][0][0]:
        dma("Y", v("W", abase(1), abase(1) + 4096), v("ar", 0, 4096), [len(OPS) - 1])
    t0 = tbase(t, h)
    for lo, hi in pieces(32 * n):
        move(v("W", t0 + lo, t0 + hi), ind(v("W", w0, abase(t) + AS), sub(slot("U", h, 4, 2), lo // 16, hi // 16)))
        scan(v("SO%d" % h, lo, hi), v("m32", 0, hi - lo), v("W", t0 + lo, t0 + hi))


def verdict(t, h):
    n = NG[h]
    nb = n // 16
    s0 = CH[h][0]
    t0 = tbase(t, h)
    ps, pa = "PS%d" % h, "PA%d" % h
    z = v("SO%d" % h, 31, 32 * n, 32)
    G, AA = slot("G", h, 0, 16), slot("A", h, 0, 16)
    si, u, uu, p = [slot("I", h, k) for k in range(4)]
    mm([(v(ps, 0, n), v("wj", 128 * t, 128 * t + 128), z)])
    copy(si, v(ps, 0, n))
    ts(u, si, 4095, ALU.bitwise_and)
    ts(own(h, 0), u, KAP[t], ALU.add)
    tt(uu, u, own(h, 0), ALU.mult)
    ts(p, uu, 5, ALU.arith_shift_right, 2047, ALU.bitwise_and)
    copy(slot("U", h, 3), p)
    if t < RO - 1:
        asel(v("zc%d" % t, 32 * s0, 32 * s0 + n), z, [[0, n]], ALU.is_ge, 0, 0)
        if h == CFG["order"][t][-1]:
            memory_write(t, h)
    gather(G, v("M%d" % t, 0, 2048), slot("U", h, 3))
    dm = v(ps, 3 * n, 4 * n)
    sums(dm, [], diffs(h, z, G, AA))
    hit = slot("X", h, 6)
    act(hit, dm, ACT.Relu, bias=col("PR%d" % t, 3), scale=1.0 / ES)

    def new(r, b):
        lo = t0 + 512 * b + place(r, h, b)
        return v("W", lo, lo + 15 * 32 + 1, 32)
    cb, sn = v(pa, 0, n), v(pa, n, 3 * n)
    c0 = (t0 % 4096) // 32
    pre = [(cb, IDN, v("c32", c0, c0 + n))]
    post = [(cb, BK, hit)]
    if t < RO - 1:
        pre += [(cb, IDN, v("cst", 64 * t, 64 * t + n))]
        pre += [(sub(sn, n * j + 16 * b, n * j + 16 * b + 16), w, new(t + 1, b))
                for j, w in enumerate((WB, WL)) for b in range(nb)]
        post += [(sub(sn, n * j, n * j + n), BK, hit) for j in range(2)]
    mm(pre, True, False)
    mm(post, False, True)
    beta = v("b0", 32 * s0, 32 * s0 + n) if t == 0 else slot("F", h, 0)
    if t < RO - 1:
        if s0 <= t < s0 + CH[h][1]:
            ta, lst = v("F%d" % h, 12 * n, 12 * n + 32), v("U%d" % h, 6 * n, 6 * n + 64)
            tt(ta, sub(cb, 32 * (t - s0), 32 * (t - s0) + 32), v("ba", 32 * t, 32 * t + 32), ALU.min)
            places(lst, [ta, ta], t0)
        tt(slot("I", h, 5, 2), sn, slot("F", h, 2, 2), ALU.min)
        tt(slot("F", h, 0), beta, cb, ALU.min)
        if s0 <= t < s0 + CH[h][1]:
            archive_write(t, v("W", t0, abase(t) + AS), lst)
        k = RO - 1 - t
        lo, hi = v(ps, 4 * n, (4 + k) * n), v(ps, 6 * n, (6 + k) * n)
        mm([(sub(reg, n * j + 16 * b, n * j + 16 * b + 16), IDN, new(t + 1 + j, b))
            for reg in (lo, hi) for j in range(k) for b in range(nb)] +
           [(sub(reg, n * j, n * j + n), mat, hit) for reg, mat in ((lo, BK), (hi, BKN)) for j in range(k)])
        old, sel = (slot("X", h, 1, 2), slot("X", h, 3, 2)) if t == 0 else (slot("X", h, 4), slot("X", h, 5))
        tt(sel, old, lo, ALU.min)
        tt(sel, sel, hi, ALU.max)
    else:
        lst = slot("U", h, 8, 2)
        tt(beta, beta, cb, ALU.min)
        places(lst, [beta, beta], t0)
        k = 16 // CFG["ypiece"]
        for r0 in range(0, 16, k):
            for b in range(nb):
                c = 32 * gene0(h, b)
                part = v("SO%d" % h, 512 * b + 32 * r0, 512 * b + 32 * (r0 + k))
                move(part, ind(v("W", t0, AOFF), sub(lst, 32 * b + 2 * r0, 32 * b + 2 * r0 + 2 * k)))
                move(rows("Y", r0, r0 + k, c, c + 32), part, CFG["gy"])
            if h == CFG["order"][t][-1]:
                dma("Y", v("y", 256 * r0, 256 * (r0 + k)), rows("Y", r0, r0 + k, 0, 256))


def memory_write(t, h):
    zc, so = "zc%d" % t, "so%d" % t
    sc = v("PS%d" % h, NG[h], NG[h] + 8)
    mm([(sc, zsel("zw", 144 * t, r), v(zc, r, 128, 16)) for r in range(16)])
    copy(v("si", 0, 8), sc)
    ts(v("si", 8, 16), v("si", 0, 8), 2047, ALU.bitwise_and)
    tt(v("sf", 0, 8), v("si", 8, 16), v("q8", 0, 8), ALU.add)
    ts(v(so, 0, 8), v("sf", 0, 8), R8, ALU.add)
    lands = [(1, 0), (2, 1)] if t == 0 else [(1, 2)]
    backs = [b for b, k in lands]
    a = send(v(zc, 0, 128), [(b, v("zl%d" % k, 0, 128), "az%d" % k) for b, k in lands], 32768)
    b2 = send(v(so, 0, 8), [(b, v("sl%d" % k, 0, 8), "az%d" % k) for b, k in lands], 2048)
    if t == 0:
        s = send(v("Mo", 0, 2048), [(3, v("M2", 0, 2048), "am2")], 1 << 19, after=[b2])
        arrive("am2", [v("M2", 0, 2048)], [(3, [3])], [s])
    for b, k in lands:
        arrive("az%d" % k, [v("zl%d" % k, 0, 128), v("sl%d" % k, 0, 8)], [(b, backs), (b, backs)], [a, b2])
        copy(ind(v("M%d" % (1 if k == 0 else 2), 0, 2048), v("sl%d" % k, 0, 8)), v("zl%d" % k, 0, 128))


def archive_write(t, win, lst):
    nxt = abase(t + 1)
    dst = [(i, nxt + 32 * (8 * (i % 16) + 4 * (i // 16) + t)) for i in range(32)]
    if t == 0:
        dst.append((0, nxt + 4096))
    if CFG["arch"] == "tmp":
        gather(v("tmp", 0, 1024), win, lst)
    for i, a0 in dst:
        if CFG["arch"] == "tmp":
            move(v("W", a0, a0 + 32), v("tmp", 32 * i, 32 * i + 32), CFG["gcopy"])
        else:
            move(v("W", a0, a0 + 32), ind(win, sub(lst, 2 * i, 2 * i + 2)))
    if t == 0:
        dma("Y", v("W", abase(2), abase(2) + AS), v("W", nxt, nxt + AS))


def build():
    setup()
    for t in range(RO):
        for h in CFG["order"][t]:
            TAG[0] = (t, h)
            flanks(t, h)
        for h in CFG["order"][t]:
            TAG[0] = (t, h)
            verdict(t, h)
    seen = {}
    for o in OPS:
        dep = dict([(d, False) for d in o["after"]] + [(d, True) for d in o.get("wait", [])])
        acc = [(x, cols(x), False) for x in o["r"]] + [(x, cols(x), True) for x in o["w"]]
        for x, m, wr in acc:
            ps = where(x) == "psum"
            for (j, mj, wj) in seen.get(x[0], []):
                e = OPS[j]["eng"]
                if ps and e == "P" and o["eng"] == "P":
                    dep.setdefault(j, False)
                elif (ps and e != o["eng"]) or ((wr or wj) and (m & mj)):
                    dep[j] = True
        for x, m, wr in acc:
            seen.setdefault(x[0], []).append((o["id"], m, wr))
        o["dep"] = dep
        o["succ"] = []
        for d in dep:
            OPS[d]["succ"].append(o["id"])


def price(M):
    out = []
    for o in OPS:
        if o["kind"] == "c":
            out.append(dict((e, c[0] + M["cy"] * (c[1] + M["g"] * c[2] + M["sc"] * c[3]) + M["pcy"] * c[4])
                            for e, (f, c) in o["alt"].items()))
        else:
            out.append(dict((e, c) for e, (f, c) in o["alt"].items()))
    return out


def priorities(M, cost):
    prio = [0.0] * len(OPS)
    for o in OPS[::-1]:
        span = min(cost[o["id"]].values())
        if o["kind"] == "d":
            span = M["dma"] + span / M["rate"]
        if o["kind"] == "r":
            span = M["riss"] + M["rem"] + span / M["rrate"]
        prio[o["id"]] = span + M["cross"] + max([prio[s] for s in o["succ"]] + [0.0])
    return [prio[o["id"]] - (CFG["bias"] * CFG["order"][o["tag"][0]].index(o["tag"][1]) if o["tag"] else 0.0)
            for o in OPS]


def follows(d, o):
    return d["kind"] == o["kind"] and d["kind"] in "dr" and not o["dep"][d["id"]]


def occupy(M, o, e, t, c, st):
    if o["kind"] == "d":
        st[0] = max(st[0], t + M["issue"]) + c / M["rate"]
        return t + M["issue"], st[0] + M["dma"]
    if o["kind"] == "r":
        free = t + M["riss"] + (0.0 if st[1] else M["rfirst"])
        st[1] = max(st[1], free) + c / M["rrate"]
        return free, st[1] + M["rem"]
    if o["kind"] == "x":
        return t, t
    return t + c, t + c


def schedule(prio, M, cost):
    N = len(OPS)
    delta, pen = CFG["delta"], CFG["pen"]
    left = [len(o["dep"]) for o in OPS]
    ready = [dict((e, 0.0) for e in o["alt"]) for o in OPS]
    fin = [0.0] * N
    beg = [0.0] * N
    free = dict((e, 0.0) for e in "VSPGYX")
    st = [0.0, 0.0]
    cand = [i for i in range(N) if left[i] == 0]
    order = dict((e, []) for e in "VSPGYX")
    while cand:
        t0, e = min((max(r, free[q]), q) for i in cand for q, r in ready[i].items())
        lim = t0 + delta
        able = [i for i in cand if ready[i].get(e, 1e18) <= lim]
        if e == "Y":
            pick = min(able)
        else:
            def rank(i):
                return prio[i] - (pen if e == "V" and OPS[i]["eng"] == "F" else 0.0), -i
            pick = max(able, key=rank)
            end = ready[pick][e] + CFG["slack"]
            fill = [i for i in able if max(ready[i][e], t0) + cost[i][e] <= end]
            if fill and ready[pick][e] > t0:
                pick = max(fill, key=rank)
        o = OPS[pick]
        t = max(ready[pick][e], free[e])
        beg[pick] = t
        free[e], fin[pick] = occupy(M, o, e, t, cost[pick][e], st)
        order[e].append(pick)
        cand.remove(pick)
        for j in o["succ"]:
            r = ready[j]
            for q in r:
                if follows(o, OPS[j]):
                    at = free[e]
                elif not OPS[j]["dep"][pick]:
                    at = fin[pick]
                else:
                    at = fin[pick] + (M["same"] if q == e else M["cross"])
                if at > r[q]:
                    r[q] = at
            left[j] -= 1
            if left[j] == 0:
                cand.append(j)
    return max(fin), order, beg, fin


QS = "VSPGYX"


def improve(M, cost, order, beg, moves, seed, heat):
    N = len(OPS)
    real, loose, pred, succ, above = [], [], [], [set() for o in OPS], []
    for o in OPS:
        cover, mine = 0, []
        for d in sorted(o["dep"], reverse=True):
            if not cover >> d & 1:
                mine.append(d)
                if o["dep"][d]:
                    cover |= above[d]
        above.append(cover | sum(1 << d for d in o["dep"] if o["dep"][d] and not cover >> d & 1))
        real.append([d for d in mine if o["dep"][d]])
        loose.append([d for d in mine if not o["dep"][d] and not follows(OPS[d], o)])
        pred.append(set(mine))
        for d in mine:
            succ[d].add(o["id"])
    same, cross = M["same"], M["cross"]
    plain = [o["kind"] in "cx" for o in OPS]
    cst = [[c.get(e, 0.0) for e in QS] for c in cost]
    tail = [0.0] * N
    for i in range(N - 1, -1, -1):
        tail[i] += min(cost[i].values()) if plain[i] else 0.0
        for d in real[i]:
            tail[d] = max(tail[d], tail[i] + min(same, cross))
        for d in loose[i]:
            tail[d] = max(tail[d], tail[i])
    eng = [0] * N
    for e in order:
        for i in order[e]:
            eng[i] = QS.index(e)
    lst, seen = [], set()

    def put(i):
        if i not in seen:
            seen.add(i)
            for d in sorted(pred[i]):
                put(d)
            lst.append(i)
    for i in sorted(range(N), key=lambda i: (beg[i], i)):
        put(i)
    alts = [[QS.index(e) for e in sorted(o["alt"])] for o in OPS]

    def run(p0, limit, fin, why, snaps):
        k = p0 >> 4
        free, last, st, top = [x[:] for x in snaps[k]]
        top = top[0]
        for p in range(k << 4, N):
            if not p & 15:
                snaps[p >> 4] = (free[:], last[:], st[:], [top])
            i = lst[p]
            e = eng[i]
            t, w = free[e], last[e]
            for d in real[i]:
                a = fin[d] + (same if eng[d] == e else cross)
                if a > t:
                    t, w = a, d
            for d in loose[i]:
                if fin[d] > t:
                    t, w = fin[d], d
            if t + tail[i] > limit:
                return None
            why[i], last[e] = w, i
            if plain[i]:
                t += cst[i][e]
                free[e] = t
            else:
                free[e], t = occupy(M, OPS[i], e, t, cst[i][e], st)
            fin[i] = t
            if t > top:
                top = t
        return top if top <= limit else None

    def longest(fin, why):
        i, way = fin.index(max(fin)), []
        while i >= 0:
            way.append(i)
            i = why[i]
        return way
    fin, why = [0.0] * N, [-1] * N
    snaps = [([0.0] * 6, [-1] * 6, [0.0, 0.0], [0.0])] * (N // 16 + 1)
    cur = run(0, 1e18, fin, why, snaps)
    way = longest(fin, why)
    best = (cur, lst[:], eng[:])
    s = seed
    for it in range(moves):
        r = []
        for k in range(5):
            s = (s * 1103515245 + 12345) & 0x7FFFFFFF
            r.append((s >> 4) / float(1 << 27))
        if r[0] < 0.8:
            i = way[int(r[1] * len(way))]
            p = lst.index(i)
        else:
            p = int(r[1] * N)
            i = lst[p]
        e = old = eng[i]
        if r[2] < 0.35:
            e = alts[i][int(r[2] / 0.35 * len(alts[i]))]
        k = int(-math.log(1.0 - r[3]) / 0.45) + (e == old)
        q = p
        if s >> 12 & 1:
            stop = pred[i]
            while q > 0 and k and lst[q - 1] not in stop:
                q -= 1
                k -= eng[lst[q]] == e
        else:
            stop = succ[i]
            while q < N - 1 and k and lst[q + 1] not in stop:
                q += 1
                k -= eng[lst[q]] == e
        if q == p and e == old:
            continue
        del lst[p]
        lst.insert(q, i)
        eng[i] = e
        f2, w2, s2 = fin[:], why[:], snaps[:]
        warm = heat[0] * (heat[1] / heat[0]) ** (it / float(moves))
        c = run(min(p, q), cur - warm * math.log(1.0 - r[4]), f2, w2, s2)
        if c is None:
            del lst[q]
            lst.insert(p, i)
            eng[i] = old
        else:
            cur, fin, why, snaps = c, f2, w2, s2
            way = longest(fin, why)
            if cur < best[0]:
                best = (cur, lst[:], eng[:])
    return best[0], dict((e, [i for i in best[1] if QS[best[2][i]] == e]) for e in QS)


def plan():
    cost = price(MODEL)
    end, order, beg, fin = schedule(priorities(MODEL, cost), MODEL, cost)
    return improve(MODEL, cost, order, beg, CFG["moves"], CFG["seed"], CFG["heat"])


build()
PLAN = [plan()]


def rank_program(g, core, T, topo):
    rank = T.rank_of(core)
    if rank is None:
        return
    c = {"g": g, "T": T, "topo": topo, "rank": rank, "core": core, "sent": [0]}
    order = PLAN[0][1]
    queue = {"V": g.vector, "S": g.scalar, "P": g.tensor, "G": g, "Y": g.sync}
    mark = {}
    total = {}
    for e in "VSPG":
        k = 0
        for i in order[e]:
            if OPS[i]["kind"] == "c":
                k += 1
                mark[i] = ("c" + e, k)
        total["c" + e] = k
    for o in OPS:
        if o["kind"] in "dx":
            mark[o["id"]] = (o["sem"], 16 if o["kind"] == "d" else arrival_count(c, o["sem"]))
            total[o["sem"]] = mark[o["id"]][1]
    done = {}
    for e in "YSGPV":
        q = queue[e]
        seen = {}
        for i in order[e]:
            o = OPS[i]
            need = {}
            for d, real in o["dep"].items():
                if real and d in mark:
                    s, k = mark[d]
                    need[s] = max(need.get(s, 0), k)
            for s, k in sorted(need.items()):
                if seen.get(s, 0) < k:
                    q.wait_ge(T.sem[s], k)
                    seen[s] = k
                    done[s] = max(done.get(s, 0), k)
            ins = o["alt"][e][0](c)
            if o["kind"] == "c":
                ins.then_inc(T.sem["c" + e], 1)
            elif o["kind"] == "d":
                ins.then_inc(T.sem[o["sem"]], 16)
    total["sent"] = c["sent"][0]
    for s, k in sorted(total.items()):
        if done.get(s, 0) < k:
            g.sync.wait_ge(T.sem[s], k)
